import numpy as np
import ml_dtypes


def mxq(x, axis, fmt="e4m3"):
    dtype, down = {"e4m3": (ml_dtypes.float8_e4m3fn, 7), "e5m2": (ml_dtypes.float8_e5m2, 14)}[fmt]
    v = np.moveaxis(np.asarray(x, np.float32).astype(ml_dtypes.bfloat16).astype(np.float64), axis, -1)
    blocks = v.reshape(v.shape[:-1] + (-1, 32))
    amax = np.abs(blocks).max(-1, keepdims=True)
    byte = np.maximum(np.where(amax > 0, np.frexp(amax)[1] - 1 + 127, 0) - down, 1)
    scale = np.exp2(byte - 127.0)
    codes = (blocks / scale).astype(np.float32).astype(dtype).astype(np.float64)
    return np.moveaxis((codes * scale).reshape(v.shape), -1, axis)


WIDE = False


def mx_kscale(k):
    if not WIDE:
        return np.ones(k)
    levels = np.array([10, -10, 5, -5, 0])
    if k % 512:
        return np.exp2(np.random.permutation(np.resize(levels, k // 32))).repeat(32)
    a = np.empty((k // 512, 16))
    for p in range(k // 512):
        a[p, :8] = np.random.permutation(np.resize(levels, 8))
        for g in range(8):
            far = levels[np.abs(levels - a[p, g]) >= 10]
            a[p, g + 8] = far[np.random.randint(len(far))]
    return np.exp2(a.ravel()).repeat(32)


def f64(x):
    return np.asarray(x).astype(np.float64)


def striped(idx):
    return np.tile(idx.reshape(-1, 16).T, (8, 1)).astype(np.uint16)


def unstriped(offs):
    return offs[:16].T.reshape(-1).astype(np.int64)


E2M1 = np.array([0.0, 0.5, 1.0, 1.5, 2.0, 3.0, 4.0, 6.0, -0.0, -0.5, -1.0, -1.5, -2.0, -3.0, -4.0, -6.0])


def pack_weight(w, fmt):
    k, n = w.shape
    w = f64(np.asarray(w, np.float32).astype(ml_dtypes.bfloat16)).reshape(k // 32, 32, n)
    amax = np.abs(w).max(1)
    if fmt == "e4m3":
        byte = np.frexp(amax)[1] - 1 + 127 - 7
    else:
        mant, ex = np.frexp(amax / 6.0)
        byte = np.where(mant > 0.5, ex, ex - 1) + 127
    byte = np.clip(np.where(amax > 0, byte, 1), 1, 254)
    scaled = (w * np.exp2(127.0 - byte)[:, None, :]).reshape(k, n).astype(np.float32)
    by_word = np.ascontiguousarray(scaled.reshape(k // 512, 128, 4, n).transpose(0, 1, 3, 2))
    if fmt == "e4m3":
        words = by_word.astype(ml_dtypes.float8_e4m3fn).view(np.uint8)
    else:
        c = by_word.astype(ml_dtypes.float4_e2m1fn).view(np.uint8) & 0xF
        words = (c[..., 0::2] | (c[..., 1::2] << 4)).reshape(k // 512, 128, 2 * n)
    return np.ascontiguousarray(words), np.ascontiguousarray(byte.astype(np.uint8).reshape(k // 512, 16, n))


def unpack_weight(words, scales, fmt):
    g, _, n = scales.shape
    words = np.ascontiguousarray(words).reshape(g, 128, n, -1)
    if fmt == "e4m3":
        vals = words.view(ml_dtypes.float8_e4m3fn).astype(np.float64)
    else:
        nib = np.empty((g, 128, n, 4), np.uint8)
        nib[..., 0::2] = words & 0xF
        nib[..., 1::2] = words >> 4
        vals = E2M1[nib]
    vals = vals * np.repeat(np.exp2(scales.astype(np.float64) - 127.0), 8, axis=1)[..., None]
    return vals.transpose(0, 1, 3, 2).reshape(g * 512, n)


def gelu(v):
    return 0.5 * v * (1.0 + np.tanh(np.sqrt(2.0 / np.pi) * (v + 0.044715 * v**3)))


K, H, N, T, S, T2 = 1024, 512, 512, 2048, 1024, 2048


def setup_inputs():
    n = np.random.standard_normal
    s = mx_kscale(K)[:, None]
    u = mx_kscale(H)[:, None]
    tab_words, tab_scales = pack_weight(n((K, T)) * s, "e4m3")
    wa4_words, wa4_scales = pack_weight(n((K, H)) / s * u.T / np.sqrt(K), "e2m1")
    wb = (n((K, H)) / s * u.T / np.sqrt(K)).astype(np.float32)
    ua = (n((H, N)) / u * np.sqrt(2.0 / H)).astype(np.float32)
    ub8_words, ub8_scales = pack_weight(n((H, N)) / u * np.sqrt(2.0 / H), "e4m3")
    wgo = np.exp(0.3 * n((128, S))).astype(np.float32)
    offs = striped(np.random.permutation(T)[:S])
    offs2 = striped(np.random.permutation(T2)[:S])
    return dict(tab_words=tab_words, tab_scales=tab_scales, offs=offs,
                wa4_words=wa4_words, wa4_scales=wa4_scales, wb=wb, ua=ua,
                ub8_words=ub8_words, ub8_scales=ub8_scales, wgo=wgo, offs2=offs2)


def reference(tab_words, tab_scales, offs, wa4_words, wa4_scales, wb, ua,
              ub8_words, ub8_scales, wgo, offs2):
    v = unpack_weight(tab_words, tab_scales, "e4m3")[:, unstriped(offs)]
    ha = np.maximum(unpack_weight(wa4_words, wa4_scales, "e2m1").T @ v, 0.0)
    hb = np.maximum(mxq(f64(wb), 0, "e4m3").T @ v, 0.0)
    ya = mxq(f64(ua), 0, "e4m3").T @ mxq(ha, 0, "e4m3")
    yb = unpack_weight(ub8_words, ub8_scales, "e4m3").T @ mxq(hb, 0, "e4m3")
    y = np.minimum(ya, yb)
    out = np.zeros((N, T2))
    out[:, unstriped(offs2)] = np.tile(f64(wgo), (N // 128, 1)) * y
    return out

@@ -1,0 +1,212 @@
+from contextlib import ExitStack
+
+import concourse.mybir as mybir
+
+K, H, N, T, S, T2 = 1024, 512, 512, 2048, 1024, 2048
+FLOPS = 2 * S * (2 * K * H + 2 * H * N)
+
+F32 = mybir.dt.float32
+BF16 = mybir.dt.bfloat16
+I32 = mybir.dt.int32
+U32 = mybir.dt.uint32
+U16 = mybir.dt.uint16
+U8 = mybir.dt.uint8
+FP8X4 = mybir.dt.float8_e4m3fn_x4
+FP4X4 = mybir.dt.float4_e2m1fn_x4
+ACT = mybir.ActivationFunctionType
+ALU = mybir.AluOpType
+
+P = 128
+PACK = 4
+KP = P * PACK
+JB = 128
+
+
+def tile_list_twin_critic_replay_kernel(tc, tab_words, tab_scales, offs, wa4_words, wa4_scales, wb, ua,
+                                                 ub8_words, ub8_scales, wgo, offs2, out):
+    nc = tc.nc
+    with ExitStack() as ctx:
+        keep = ctx.enter_context(tc.tile_pool(name="keep", bufs=1))
+        ring = ctx.enter_context(tc.tile_pool(name="ring", bufs=3))
+        ps1 = ctx.enter_context(tc.psum_pool(name="ps1", bufs=4))
+        ps2 = ctx.enter_context(tc.psum_pool(name="ps2", bufs=2))
+
+        def kt(shape, dtype, name):
+            return keep.tile(shape, dtype, name=name, align_bytes=64)
+
+        idx = keep.tile([P, S // 16], U16, name="idx")
+        idx2 = keep.tile([P, S // 16], U16, name="idx2")
+        tabw = [kt([P, T], I32, "tabw%d" % a) for a in range(2)]
+        tabs = kt([P, T], U8, "tabs")
+        vw = [kt([P, S], U32, "vw%d" % a) for a in range(2)]
+        vs = kt([P, S], U8, "vs")
+        vs1 = kt([P, S], U8, "vs1")
+        wa_raw = kt([P, 2, 2 * H], U8, "wa_raw")
+        wa_w = kt([P, 2, 2 * H], U8, "wa_w")
+        was_raw = kt([P, 2, H], U8, "was_raw")
+        wa_s = kt([P, 2, H], U8, "wa_s")
+        wb_raw = [[kt([P, PACK, H // 2], F32, "wb_raw%d%d" % (a, h)) for h in range(2)] for a in range(2)]
+        wb_bf = [kt([P, PACK * H], BF16, "wb_bf%d" % a) for a in range(2)]
+        wb_w = [kt([P, H], U32, "wb_w%d" % a) for a in range(2)]
+        wb_s = [kt([P, H], U8, "wb_s%d" % a) for a in range(2)]
+        ua_first = kt([P, PACK, 2 * P], F32, "ua_first")
+        ua_rest = kt([P, PACK, N - 2 * P], F32, "ua_rest")
+        ua_bf = kt([P, PACK * N], BF16, "ua_bf")
+        ua_w = kt([P, N], U32, "ua_w")
+        ua_s = kt([P, N], U8, "ua_s")
+        ub_w = kt([P, N], I32, "ub_w")
+        ub_s = kt([P, N], U8, "ub_s")
+        h_bf = [kt([P, PACK * S], BF16, "h_bf%d" % b) for b in range(2)]
+        h_w = [kt([P, S], U32, "h_w%d" % b) for b in range(2)]
+        h_s = [kt([P, S], U8, "h_s%d" % b) for b in range(2)]
+        page = [kt([P, T2], F32, "page%d" % i) for i in range(2)]
+        wgt = kt([P, S], F32, "wgt")
+
+        nc.gpsimd.memset(tabs[:].bitcast(I32), 0)
+        nc.gpsimd.memset(was_raw[:].rearrange("p a c -> p (a c)").bitcast(I32), 0)
+        nc.gpsimd.memset(vs1[:].bitcast(I32), 0)
+        nc.gpsimd.memset(ub_s[:].bitcast(I32), 0)
+        for i in range(2):
+            nc.vector.memset(page[i][:], 0.0)
+
+        def load_words(a):
+            nc.sync.dma_start(tabw[a][:], tab_words[a].rearrange("p t i -> p (t i)").bitcast(I32))
+
+        def load_wb(a, h):
+            cols = slice(h * H // 2, (h + 1) * H // 2)
+            nc.sync.dma_start(wb_raw[a][h][:], wb[a * KP:(a + 1) * KP, cols].rearrange("(p j) c -> p j c", j=PACK))
+
+        nc.sync.dma_start(idx[:], offs)
+        load_words(0)
+        for q in range(4):
+            nc.sync.dma_start(tabs[32 * q:32 * q + 8, :].bitcast(I32), tab_scales[:, 4 * q:4 * q + 4, :].bitcast(I32))
+        load_wb(0, 0)
+        load_wb(0, 1)
+        nc.sync.dma_start(wa_raw[:].bitcast(I32), wa4_words.rearrange("a p c -> p a c").bitcast(I32))
+        load_words(1)
+        for q in range(4):
+            nc.sync.dma_start(was_raw[32 * q:32 * q + 4, :, :].bitcast(I32),
+                              wa4_scales[:, 4 * q:4 * q + 4, :].rearrange("a r c -> r a c").bitcast(I32))
+        load_wb(1, 0)
+        load_wb(1, 1)
+        ua_v = ua.rearrange("(p j) n -> p j n", j=PACK)
+        nc.sync.dma_start(ua_first[:], ua_v[:, :, 0:2 * P])
+        nc.sync.dma_start(ub_w[:], ub8_words[0].rearrange("p c i -> p (c i)").bitcast(I32))
+        for q in range(4):
+            nc.sync.dma_start(ub_s[32 * q:32 * q + 4, :].bitcast(I32), ub8_scales[0, 4 * q:4 * q + 4, :].bitcast(I32))
+        nc.sync.dma_start(idx2[:], offs2)
+        nc.sync.dma_start(wgt[:, 0:S // 2], wgo[:, 0:S // 2])
+        nc.sync.dma_start(ua_rest[:], ua_v[:, :, 2 * P:N])
+        nc.sync.dma_start(wgt[:, S // 2:S], wgo[:, S // 2:S])
+
+        def gather_words(a, j0, j1):
+            nc.vector.tensor_copy(vw[a][:, j0:j1], tabw[a][:].bitcast(U32).indirect(idx[:, j0 // 16:j1 // 16]))
+
+        def cast_wb(a, h):
+            dst = wb_bf[a][:].rearrange("p (t m j) -> p m t j", t=PACK, j=PACK)[:, h * P // 2:(h + 1) * P // 2, :, :]
+            nc.scalar.activation(dst, wb_raw[a][h][:].rearrange("p j (m t) -> p m t j", t=PACK), ACT.Copy)
+
+        def quant_wb(a):
+            nc.vector.quantize_mx(out=wb_w[a][:].bitcast(FP8X4), scales=wb_s[a][:], in_=wb_bf[a][:])
+
+        def cast_ua(nt):
+            raw = ua_first[:, :, nt * P:(nt + 1) * P] if nt < 2 else ua_rest[:, :, (nt - 2) * P:(nt - 1) * P]
+            dst = ua_bf[:, nt * KP:(nt + 1) * KP].rearrange("p (c i j) -> p c j i", i=4, j=PACK)
+            nc.scalar.activation(dst, raw.rearrange("p j (c i) -> p c j i", i=4), ACT.Copy)
+
+        def quant_ua(nt):
+            cols = slice(nt * P, (nt + 1) * P)
+            nc.vector.quantize_mx(out=ua_w[:, cols].bitcast(FP8X4), scales=ua_s[:, cols],
+                                  in_=ua_bf[:, nt * KP:(nt + 1) * KP])
+
+        def hidden(b, jb):
+            js = slice(jb * JB, (jb + 1) * JB)
+            bank = ps1.tile([P, PACK, JB], F32, name="bank")
+            for t in range(PACK):
+                for a in range(2):
+                    cols = slice(t * P, (t + 1) * P)
+                    if b == 0:
+                        lhs = wa_w[:, a, 2 * t * P:2 * (t + 1) * P].bitcast(FP4X4)
+                        lhs_s = wa_s[:, a, cols]
+                        rhs_s = vs[:, js] if a == 0 else vs1[:, js]
+                    else:
+                        lhs = wb_w[a][:, cols].bitcast(FP8X4)
+                        lhs_s = wb_s[a][:, cols]
+                        rhs_s = vs[4 * a:P, js]
+                    nc.tensor.matmul_mx(out=bank[:, t, :], lhsT=lhs, lhsT_scale=lhs_s, rhs=vw[a][:, js].bitcast(FP8X4),
+                                        rhs_scale=rhs_s, start=(a == 0), stop=(a == 1))
+            dst = h_bf[b][:, jb * KP:(jb + 1) * KP].rearrange("p (n t) -> p n t", t=PACK)
+            nc.scalar.activation(dst, bank[:].rearrange("p t n -> p n t"), ACT.Relu)
+
+        def quant_h(b, j0, j1):
+            nc.vector.quantize_mx(out=h_w[b][:, j0:j1].bitcast(FP8X4), scales=h_s[b][:, j0:j1],
+                                  in_=h_bf[b][:, PACK * j0:PACK * j1])
+
+        def values(nt, j0, j1, y, y0):
+            cols = slice(nt * P, (nt + 1) * P)
+            n = j1 - j0
+            ya = ps2.tile([P, 512], F32, name="ya")
+            yb = ps2.tile([P, 512], F32, name="yb")
+            nc.tensor.matmul_mx(out=ya[:, 0:n], lhsT=ua_w[:, cols].bitcast(FP8X4), lhsT_scale=ua_s[:, cols],
+                                rhs=h_w[0][:, j0:j1].bitcast(FP8X4), rhs_scale=h_s[0][:, j0:j1], start=True, stop=True)
+            nc.tensor.matmul_mx(out=yb[:, 0:n], lhsT=ub_w[:, cols].bitcast(FP8X4), lhsT_scale=ub_s[:, cols],
+                                rhs=h_w[1][:, j0:j1].bitcast(FP8X4), rhs_scale=h_s[1][:, j0:j1], start=True, stop=True)
+            ya_sb = ring.tile([P, 512], F32, name="ya_sb")
+            nc.scalar.copy(ya_sb[:, 0:n], ya[:, 0:n])
+            nc.vector.tensor_tensor(y[:, j0 - y0:j1 - y0], yb[:, 0:n], ya_sb[:, 0:n], ALU.min)
+
+        def scatter(nt, j0, j1, y):
+            nc.vector.tensor_tensor(page[nt % 2][:].indirect(idx2[:, j0 // 16:j1 // 16]), y[:, 0:j1 - j0],
+                                    wgt[:, j0:j1], ALU.mult)
+
+        gather_words(0, 0, 512)
+        nc.vector.tensor_copy(vs[:], tabs[:].indirect(idx[:]))
+        nc.scalar.dma_start(vs1[0:112, :].bitcast(I32), vs[4:116, :].bitcast(I32))
+        cast_wb(0, 0)
+        cast_wb(0, 1)
+        nc.vector.tensor_copy(
+            wa_w[:].bitcast(U16).rearrange("p a (t o i) -> p a o t i", t=PACK, i=8),
+            wa_raw[:].bitcast(U16).rearrange("p a (o i t) -> p a o t i", t=PACK, i=8))
+        gather_words(0, 512, S)
+        quant_wb(0)
+        nc.vector.tensor_copy(
+            wa_s[:].rearrange("p a (t o i) -> p a o t i", t=PACK, i=16),
+            was_raw[:].rearrange("p a (o i t) -> p a o t i", t=PACK, i=16))
+        spans = [(0, 256), (256, 512), (512, 1024)]
+        gather_words(1, 0, 256)
+        hidden(0, 0)
+        hidden(0, 1)
+        cast_wb(1, 0)
+        gather_words(1, 256, 512)
+        cast_wb(1, 1)
+        quant_wb(1)
+        gather_words(1, 512, 1024)
+        quant_h(0, 0, 256)
+        hidden(1, 0)
+        hidden(1, 1)
+        cast_ua(0)
+        quant_ua(0)
+        cast_ua(1)
+        quant_ua(1)
+        for j0, j1 in spans:
+            if j0 > 0:
+                for jb in range(j0 // JB, j1 // JB):
+                    hidden(0, jb)
+                quant_h(0, j0, j1)
+                for jb in range(j0 // JB, j1 // JB):
+                    hidden(1, jb)
+            quant_h(1, j0, j1)
+            for nt in range(2):
+                y = ring.tile([P, S], F32, name="y")
+                values(nt, j0, j1, y, j0)
+                scatter(nt, j0, j1, y)
+                if j1 == S:
+                    nc.sync.dma_start(out[nt * P:(nt + 1) * P, :], page[nt % 2][:])
+        for nt in range(2, N // P):
+            cast_ua(nt)
+            quant_ua(nt)
+            y = ring.tile([P, S], F32, name="y")
+            for j0 in (0, 512):
+                values(nt, j0, j0 + 512, y, 0)
+            scatter(nt, 0, S, y)
+            nc.sync.dma_start(out[nt * P:(nt + 1) * P, :], page[nt % 2][:])

@@ -28,121 +28,147 @@ def tile_list_twin_critic_replay_kernel(tc, tab_words, tab_scales, offs, wa4_wor
     with ExitStack() as ctx:
         keep = ctx.enter_context(tc.tile_pool(name="keep", bufs=1))
         ring = ctx.enter_context(tc.tile_pool(name="ring", bufs=3))
+        reuse = ctx.enter_context(tc.tile_pool(name="reuse", bufs=1))
         ps1 = ctx.enter_context(tc.psum_pool(name="ps1", bufs=4))
         ps2 = ctx.enter_context(tc.psum_pool(name="ps2", bufs=2))
 
         def kt(shape, dtype, name):
             return keep.tile(shape, dtype, name=name, align_bytes=64)
 
+        def rt(shape, dtype, name, offset):
+            return reuse.tile(shape, dtype, name=name, align_bytes=64, offset=offset)
+
+        SP = 256
+        CUT = 192
         idx = keep.tile([P, S // 16], U16, name="idx")
         idx2 = keep.tile([P, S // 16], U16, name="idx2")
-        tabw = [kt([P, T], I32, "tabw%d" % a) for a in range(2)]
-        tabs = kt([P, T], U8, "tabs")
-        vw = [kt([P, S], U32, "vw%d" % a) for a in range(2)]
-        vs = kt([P, S], U8, "vs")
-        vs1 = kt([P, S], U8, "vs1")
+        tabw = [rt([P, T], I32, "tabw0", 4096), kt([P, T], I32, "tabw1")]
+        tabs = rt([P, T], U8, "tabs", 20032)
+        vw0 = kt([P, S], U32, "vw0")
+        vw1 = [kt([P, SP], U32, "vw1_%d" % s) for s in range(2)]
+        vs_top = kt([P, S], U8, "vs_top")
+        vs = kt([P, 2, S], U8, "vs")
         wa_raw = kt([P, 2, 2 * H], U8, "wa_raw")
         wa_w = kt([P, 2, 2 * H], U8, "wa_w")
         was_raw = kt([P, 2, H], U8, "was_raw")
-        wa_s = kt([P, 2, H], U8, "wa_s")
-        wb_raw = [[kt([P, PACK, H // 2], F32, "wb_raw%d%d" % (a, h)) for h in range(2)] for a in range(2)]
+        wa_s = rt([P, 2, H], U8, "wa_s", 10304)
+        wb_first = kt([P, PACK, H], F32, "wb_first")
+        wb_last = rt([P, PACK, H], F32, "wb_last", 20032)
         wb_bf = [kt([P, PACK * H], BF16, "wb_bf%d" % a) for a in range(2)]
         wb_w = [kt([P, H], U32, "wb_w%d" % a) for a in range(2)]
         wb_s = [kt([P, H], U8, "wb_s%d" % a) for a in range(2)]
-        ua_first = kt([P, PACK, 2 * P], F32, "ua_first")
-        ua_rest = kt([P, PACK, N - 2 * P], F32, "ua_rest")
+        ua_raw = [rt([P, PACK, 2 * P], F32, "ua_raw0", 64)]
         ua_bf = kt([P, PACK * N], BF16, "ua_bf")
         ua_w = kt([P, N], U32, "ua_w")
         ua_s = kt([P, N], U8, "ua_s")
-        ub_w = kt([P, N], I32, "ub_w")
-        ub_s = kt([P, N], U8, "ub_s")
-        h_bf = [kt([P, PACK * S], BF16, "h_bf%d" % b) for b in range(2)]
+        ub_w = rt([P, N], I32, "ub_w", 4160)
+        ub_s = rt([P, N], U8, "ub_s", 11328)
+        wgt = rt([P, S], F32, "wgt", 6208)
+        h_bf = [[rt([P, PACK * SP], BF16, "h_bf01", 24128) if (b, s) == (0, 1) else
+                 kt([P, PACK * SP], BF16, "h_bf%d%d" % (b, s)) for s in range(S // SP)] for b in range(2)]
         h_w = [kt([P, S], U32, "h_w%d" % b) for b in range(2)]
         h_s = [kt([P, S], U8, "h_s%d" % b) for b in range(2)]
-        page = [kt([P, T2], F32, "page%d" % i) for i in range(2)]
-        wgt = kt([P, S], F32, "wgt")
+        page = [kt([P, T2], F32, "page0"), rt([P, T2], F32, "page1", 11840)]
 
-        nc.gpsimd.memset(tabs[:].bitcast(I32), 0)
+        for q in range(4):
+            nc.vector.memset(tabs[32 * q:32 * q + 24, :].bitcast(I32), 0)
         nc.gpsimd.memset(was_raw[:].rearrange("p a c -> p (a c)").bitcast(I32), 0)
-        nc.gpsimd.memset(vs1[:].bitcast(I32), 0)
-        nc.gpsimd.memset(ub_s[:].bitcast(I32), 0)
-        for i in range(2):
-            nc.vector.memset(page[i][:], 0.0)
+        for q in range(4):
+            nc.scalar.dma_start(was_raw[32 * q:32 * q + 4, :, :].bitcast(I32),
+                                wa4_scales[:, 4 * q:4 * q + 4, :].rearrange("a r c -> r a c").bitcast(I32))
+        nc.gpsimd.memset(vs[96:P, :, :].rearrange("p a j -> p (a j)").bitcast(I32), 0)
 
         def load_words(a):
             nc.sync.dma_start(tabw[a][:], tab_words[a].rearrange("p t i -> p (t i)").bitcast(I32))
 
-        def load_wb(a, h):
-            cols = slice(h * H // 2, (h + 1) * H // 2)
-            nc.sync.dma_start(wb_raw[a][h][:], wb[a * KP:(a + 1) * KP, cols].rearrange("(p j) c -> p j c", j=PACK))
+        def load_wb(dst, a):
+            nc.sync.dma_start(dst[:], wb[a * KP:(a + 1) * KP, :].rearrange("(p j) c -> p j c", j=PACK))
+
+        def load_ua(h):
+            rows = ua.rearrange("(g t i) n -> t g i n", t=PACK, i=8)
+            for t in range(PACK):
+                nc.sync.dma_start(ua_raw[h][:, t, :], rows[t][:, :, h * 2 * P:(h + 1) * 2 * P])
 
         nc.sync.dma_start(idx[:], offs)
-        load_words(0)
         for q in range(4):
-            nc.sync.dma_start(tabs[32 * q:32 * q + 8, :].bitcast(I32), tab_scales[:, 4 * q:4 * q + 4, :].bitcast(I32))
-        load_wb(0, 0)
-        load_wb(0, 1)
+            nc.sync.dma_start(tabs[32 * q + 24:32 * q + 32, :].bitcast(I32), tab_scales[:, 4 * q:4 * q + 4, :].bitcast(I32))
+        load_words(0)
+        load_wb(wb_first, 0)
         nc.sync.dma_start(wa_raw[:].bitcast(I32), wa4_words.rearrange("a p c -> p a c").bitcast(I32))
         load_words(1)
-        for q in range(4):
-            nc.sync.dma_start(was_raw[32 * q:32 * q + 4, :, :].bitcast(I32),
-                              wa4_scales[:, 4 * q:4 * q + 4, :].rearrange("a r c -> r a c").bitcast(I32))
-        load_wb(1, 0)
-        load_wb(1, 1)
-        ua_v = ua.rearrange("(p j) n -> p j n", j=PACK)
-        nc.sync.dma_start(ua_first[:], ua_v[:, :, 0:2 * P])
-        nc.sync.dma_start(ub_w[:], ub8_words[0].rearrange("p c i -> p (c i)").bitcast(I32))
-        for q in range(4):
-            nc.sync.dma_start(ub_s[32 * q:32 * q + 4, :].bitcast(I32), ub8_scales[0, 4 * q:4 * q + 4, :].bitcast(I32))
         nc.sync.dma_start(idx2[:], offs2)
-        nc.sync.dma_start(wgt[:, 0:S // 2], wgo[:, 0:S // 2])
-        nc.sync.dma_start(ua_rest[:], ua_v[:, :, 2 * P:N])
-        nc.sync.dma_start(wgt[:, S // 2:S], wgo[:, S // 2:S])
 
-        def gather_words(a, j0, j1):
-            nc.vector.tensor_copy(vw[a][:, j0:j1], tabw[a][:].bitcast(U32).indirect(idx[:, j0 // 16:j1 // 16]))
+        def gather_words(dst, a, j0, j1):
+            nc.vector.tensor_copy(dst, tabw[a][:].bitcast(U32).indirect(idx[:, j0 // 16:j1 // 16]))
 
-        def cast_wb(a, h):
-            dst = wb_bf[a][:].rearrange("p (t m j) -> p m t j", t=PACK, j=PACK)[:, h * P // 2:(h + 1) * P // 2, :, :]
-            nc.scalar.activation(dst, wb_raw[a][h][:].rearrange("p j (m t) -> p m t j", t=PACK), ACT.Copy)
+        def cast_wb(a, raw, c0, c1, on_vector=False):
+            dst = wb_bf[a][:].rearrange("p (t m j) -> p m t j", t=PACK, j=PACK)[:, c0 // PACK:c1 // PACK, :, :]
+            src = raw.rearrange("p j (m t) -> p m t j", t=PACK)
+            if on_vector:
+                nc.vector.tensor_copy(dst, src)
+            else:
+                nc.scalar.activation(dst, src, ACT.Copy)
 
-        def quant_wb(a):
-            nc.vector.quantize_mx(out=wb_w[a][:].bitcast(FP8X4), scales=wb_s[a][:], in_=wb_bf[a][:])
+        def quant_wb(a, c0, c1):
+            nc.vector.quantize_mx(out=wb_w[a][:, c0:c1].bitcast(FP8X4), scales=wb_s[a][:, c0:c1],
+                                  in_=wb_bf[a][:, PACK * c0:PACK * c1])
 
         def cast_ua(nt):
-            raw = ua_first[:, :, nt * P:(nt + 1) * P] if nt < 2 else ua_rest[:, :, (nt - 2) * P:(nt - 1) * P]
+            raw = ua_raw[nt // 2][:, :, (nt % 2) * P:(nt % 2 + 1) * P]
             dst = ua_bf[:, nt * KP:(nt + 1) * KP].rearrange("p (c i j) -> p c j i", i=4, j=PACK)
             nc.scalar.activation(dst, raw.rearrange("p j (c i) -> p c j i", i=4), ACT.Copy)
 
-        def quant_ua(nt):
-            cols = slice(nt * P, (nt + 1) * P)
+        def quant_ua(n0, n1):
+            cols = slice(n0 * P, n1 * P)
             nc.vector.quantize_mx(out=ua_w[:, cols].bitcast(FP8X4), scales=ua_s[:, cols],
-                                  in_=ua_bf[:, nt * KP:(nt + 1) * KP])
+                                  in_=ua_bf[:, n0 * KP:n1 * KP])
+
+        def table_words(a, jb):
+            if a == 0:
+                return vw0[:, jb * JB:(jb + 1) * JB]
+            piece = min(jb // 2, 2)
+            j0 = jb * JB - piece * SP
+            return vw1[piece][:, j0:j0 + JB]
+
+        def one_pass(b, jb, bank, a, t):
+            cols = slice(t * P, (t + 1) * P)
+            if b == 0:
+                lhs = wa_w[:, a, 2 * t * P:2 * (t + 1) * P].bitcast(FP4X4)
+                lhs_s = wa_s[:, a, cols]
+            else:
+                lhs = wb_w[a][:, cols].bitcast(FP8X4)
+                lhs_s = wb_s[a][:, cols]
+            nc.tensor.matmul_mx(out=bank[:, t, :], lhsT=lhs, lhsT_scale=lhs_s, rhs=table_words(a, jb).bitcast(FP8X4),
+                                rhs_scale=vs[:, a, jb * JB:(jb + 1) * JB],
+                                start=(a == 0 and t == 0), stop=(a == 1 and t == PACK - 1))
+
+        def relu(b, jb, bank, on_vector=False):
+            off = (jb % 2) * KP
+            dst = h_bf[b][jb // 2][:, off:off + KP].rearrange("p (n t) -> p n t", t=PACK)
+            src = bank[:].rearrange("p t n -> p n t")
+            if on_vector:
+                nc.vector.tensor_scalar_max(dst, src, 0.0)
+            else:
+                nc.scalar.activation(dst, src, ACT.Relu)
 
         def hidden(b, jb):
-            js = slice(jb * JB, (jb + 1) * JB)
             bank = ps1.tile([P, PACK, JB], F32, name="bank")
-            for t in range(PACK):
-                for a in range(2):
-                    cols = slice(t * P, (t + 1) * P)
-                    if b == 0:
-                        lhs = wa_w[:, a, 2 * t * P:2 * (t + 1) * P].bitcast(FP4X4)
-                        lhs_s = wa_s[:, a, cols]
-                        rhs_s = vs[:, js] if a == 0 else vs1[:, js]
-                    else:
-                        lhs = wb_w[a][:, cols].bitcast(FP8X4)
-                        lhs_s = wb_s[a][:, cols]
-                        rhs_s = vs[4 * a:P, js]
-                    nc.tensor.matmul_mx(out=bank[:, t, :], lhsT=lhs, lhsT_scale=lhs_s, rhs=vw[a][:, js].bitcast(FP8X4),
-                                        rhs_scale=rhs_s, start=(a == 0), stop=(a == 1))
-            dst = h_bf[b][:, jb * KP:(jb + 1) * KP].rearrange("p (n t) -> p n t", t=PACK)
-            nc.scalar.activation(dst, bank[:].rearrange("p t n -> p n t"), ACT.Relu)
+            for a in range(2):
+                for t in range(PACK):
+                    one_pass(b, jb, bank, a, t)
+            relu(b, jb, bank)
 
-        def quant_h(b, j0, j1):
-            nc.vector.quantize_mx(out=h_w[b][:, j0:j1].bitcast(FP8X4), scales=h_s[b][:, j0:j1],
-                                  in_=h_bf[b][:, PACK * j0:PACK * j1])
+        def quant_h(b, s):
+            js = slice(s * SP, (s + 1) * SP)
+            nc.vector.quantize_mx(out=h_w[b][:, js].bitcast(FP8X4), scales=h_s[b][:, js], in_=h_bf[b][s][:])
 
-        def values(nt, j0, j1, y, y0):
+        def span(s):
+            for b in range(2):
+                hidden(b, 2 * s)
+                hidden(b, 2 * s + 1)
+                quant_h(b, s)
+
+        def values(nt, j0, j1, y):
             cols = slice(nt * P, (nt + 1) * P)
             n = j1 - j0
             ya = ps2.tile([P, 512], F32, name="ya")
@@ -153,60 +179,78 @@ def tile_list_twin_critic_replay_kernel(tc, tab_words, tab_scales, offs, wa4_wor
                                 rhs=h_w[1][:, j0:j1].bitcast(FP8X4), rhs_scale=h_s[1][:, j0:j1], start=True, stop=True)
             ya_sb = ring.tile([P, 512], F32, name="ya_sb")
             nc.scalar.copy(ya_sb[:, 0:n], ya[:, 0:n])
-            nc.vector.tensor_tensor(y[:, j0 - y0:j1 - y0], yb[:, 0:n], ya_sb[:, 0:n], ALU.min)
+            nc.vector.tensor_tensor(y, yb[:, 0:n], ya_sb[:, 0:n], ALU.min)
 
         def scatter(nt, j0, j1, y):
-            nc.vector.tensor_tensor(page[nt % 2][:].indirect(idx2[:, j0 // 16:j1 // 16]), y[:, 0:j1 - j0],
-                                    wgt[:, j0:j1], ALU.mult)
+            nc.vector.tensor_tensor(page[nt % 2][:].indirect(idx2[:, j0 // 16:j1 // 16]), y, wgt[:, j0:j1], ALU.mult)
 
-        gather_words(0, 0, 512)
-        nc.vector.tensor_copy(vs[:], tabs[:].indirect(idx[:]))
-        nc.scalar.dma_start(vs1[0:112, :].bitcast(I32), vs[4:116, :].bitcast(I32))
-        cast_wb(0, 0)
-        cast_wb(0, 1)
-        nc.vector.tensor_copy(
-            wa_w[:].bitcast(U16).rearrange("p a (t o i) -> p a o t i", t=PACK, i=8),
-            wa_raw[:].bitcast(U16).rearrange("p a (o i t) -> p a o t i", t=PACK, i=8))
-        gather_words(0, 512, S)
-        quant_wb(0)
-        nc.vector.tensor_copy(
-            wa_s[:].rearrange("p a (t o i) -> p a o t i", t=PACK, i=16),
-            was_raw[:].rearrange("p a (o i t) -> p a o t i", t=PACK, i=16))
-        spans = [(0, 256), (256, 512), (512, 1024)]
-        gather_words(1, 0, 256)
+        def store(nt):
+            nc.sync.dma_start(out[nt * P:(nt + 1) * P, :], page[nt % 2][:])
+
+        nc.vector.tensor_copy(vs_top[:], tabs[:].indirect(idx[:]))
+        for a in range(2):
+            nc.sync.dma_start(vs[0:100, a, :].bitcast(I32), vs_top[24 + 4 * a:124 + 4 * a, :].bitcast(I32))
+        load_wb(wb_last, 1)
+        gather_words(vw0[:], 0, 0, S)
+        nc.vector.memset(ub_s[:].bitcast(I32), 0)
+        for i in range(2):
+            for c in range(0, T2, 512):
+                nc.vector.memset(page[i][:, c:c + 512], 0.0)
+        load_ua(0)
+        nc.sync.dma_start(ub_w[:], ub8_words[0].rearrange("p c i -> p (c i)").bitcast(I32))
+        for q in range(4):
+            nc.sync.dma_start(ub_s[32 * q:32 * q + 4, :].bitcast(I32), ub8_scales[0, 4 * q:4 * q + 4, :].bitcast(I32))
+        nc.sync.dma_start(wgt[:], wgo)
+        cast_wb(0, wb_first[:], 0, H)
+        ua_raw.append(kt([P, PACK, 2 * P], F32, "wb_first"))
+        load_ua(1)
+        for raw, put, words in ((wa_raw, wa_w, 4), (was_raw, wa_s, 2)):
+            nc.vector.tensor_copy(put[:].bitcast(I32).rearrange("p a (t g i) -> p a g t i", t=PACK, i=words),
+                                  raw[:].bitcast(I32).rearrange("p a (g t i) -> p a g t i", t=PACK, i=words))
+        gather_words(vw1[0][:], 1, 0, SP)
+        quant_wb(0, 0, H)
+        gather_words(vw1[1][:], 1, SP, 2 * SP)
         hidden(0, 0)
         hidden(0, 1)
-        cast_wb(1, 0)
-        gather_words(1, 256, 512)
-        cast_wb(1, 1)
-        quant_wb(1)
-        gather_words(1, 512, 1024)
-        quant_h(0, 0, 256)
-        hidden(1, 0)
-        hidden(1, 1)
+        quant_h(0, 0)
+        cast_wb(1, wb_last[:, :, 0:CUT], 0, CUT)
+        cast_wb(1, wb_last[:, :, CUT:H], CUT, H, True)
+        quant_wb(1, 0, H // 2)
+        quant_wb(1, H // 2, H)
+        banks = [ps1.tile([P, PACK, JB], F32, name="bank") for jb in range(2)]
+        for a in range(2):
+            for t in range(PACK):
+                for jb in range(2):
+                    one_pass(1, jb, banks[jb], a, t)
         cast_ua(0)
-        quant_ua(0)
-        cast_ua(1)
-        quant_ua(1)
-        for j0, j1 in spans:
-            if j0 > 0:
-                for jb in range(j0 // JB, j1 // JB):
-                    hidden(0, jb)
-                quant_h(0, j0, j1)
-                for jb in range(j0 // JB, j1 // JB):
-                    hidden(1, jb)
-            quant_h(1, j0, j1)
-            for nt in range(2):
-                y = ring.tile([P, S], F32, name="y")
-                values(nt, j0, j1, y, j0)
-                scatter(nt, j0, j1, y)
-                if j1 == S:
-                    nc.sync.dma_start(out[nt * P:(nt + 1) * P, :], page[nt % 2][:])
+        quant_ua(0, 1)
+        relu(1, 0, banks[0])
+        relu(1, 1, banks[1], True)
+        quant_h(1, 0)
+        vw1.append(kt([P, 2 * SP], U32, "h_bf10"))
+        gather_words(vw1[2][:], 1, 2 * SP, S)
+        for s in range(3):
+            y = ring.tile([P, S], F32, name="y")
+            values(0, s * SP, (s + 1) * SP, y[:, 0:SP])
+            scatter(0, s * SP, (s + 1) * SP, y[:, 0:SP])
+            if s == 0:
+                cast_ua(1)
+                quant_ua(1, 2)
+            span(s + 1)
+            y = kt([P, SP], F32, "h_bf1%d" % (s + 1))
+            values(1, s * SP, (s + 1) * SP, y[:])
+            scatter(1, s * SP, (s + 1) * SP, y[:])
+        for nt in range(2):
+            y = ring.tile([P, S], F32, name="y")
+            values(nt, 3 * SP, S, y[:, 0:SP])
+            scatter(nt, 3 * SP, S, y[:, 0:SP])
+            store(nt)
+        cast_ua(2)
+        cast_ua(3)
+        quant_ua(2, 4)
         for nt in range(2, N // P):
-            cast_ua(nt)
-            quant_ua(nt)
             y = ring.tile([P, S], F32, name="y")
             for j0 in (0, 512):
-                values(nt, j0, j0 + 512, y, 0)
-            scatter(nt, 0, S, y)
-            nc.sync.dma_start(out[nt * P:(nt + 1) * P, :], page[nt % 2][:])
+                values(nt, j0, j0 + 512, y[:, j0:j0 + 512])
+            scatter(nt, 0, S, y[:])
+            store(nt)

@@ -20,6 +20,8 @@ P = 128
 PACK = 4
 KP = P * PACK
 JB = 128
+SP = 256
+CUT = 192
 
 
 def tile_list_twin_critic_replay_kernel(tc, tab_words, tab_scales, offs, wa4_words, wa4_scales, wb, ua,
@@ -27,62 +29,66 @@ def tile_list_twin_critic_replay_kernel(tc, tab_words, tab_scales, offs, wa4_wor
     nc = tc.nc
     with ExitStack() as ctx:
         keep = ctx.enter_context(tc.tile_pool(name="keep", bufs=1))
-        ring = ctx.enter_context(tc.tile_pool(name="ring", bufs=3))
+        ring = ctx.enter_context(tc.tile_pool(name="ring", bufs=6))
         reuse = ctx.enter_context(tc.tile_pool(name="reuse", bufs=1))
-        ps1 = ctx.enter_context(tc.psum_pool(name="ps1", bufs=4))
-        ps2 = ctx.enter_context(tc.psum_pool(name="ps2", bufs=2))
+        psum = ctx.enter_context(tc.psum_pool(name="psum", bufs=1))
 
         def kt(shape, dtype, name):
             return keep.tile(shape, dtype, name=name, align_bytes=64)
 
         def rt(shape, dtype, name, offset):
-            return reuse.tile(shape, dtype, name=name, align_bytes=64, offset=offset)
+            return reuse.tile(shape, dtype, name=name, align_bytes=64, offset=4096 + offset)
 
-        SP = 256
-        CUT = 192
         idx = keep.tile([P, S // 16], U16, name="idx")
         idx2 = keep.tile([P, S // 16], U16, name="idx2")
         tabw = [rt([P, T], I32, "tabw0", 4096), kt([P, T], I32, "tabw1")]
-        tabs = rt([P, T], U8, "tabs", 20032)
-        vw0 = kt([P, S], U32, "vw0")
-        vw1 = [kt([P, SP], U32, "vw1_%d" % s) for s in range(2)]
+        tabs = rt([P, T], U8, "tabs", 22528)
+        vw = [kt([P, S], U32, "vw%d" % a) for a in range(2)]
         vs_top = kt([P, S], U8, "vs_top")
         vs = kt([P, 2, S], U8, "vs")
         wa_raw = kt([P, 2, 2 * H], U8, "wa_raw")
         wa_w = kt([P, 2, 2 * H], U8, "wa_w")
         was_raw = kt([P, 2, H], U8, "was_raw")
-        wa_s = rt([P, 2, H], U8, "wa_s", 10304)
-        wb_first = kt([P, PACK, H], F32, "wb_first")
-        wb_last = rt([P, PACK, H], F32, "wb_last", 20032)
+        wa_s = kt([P, 2, H], U8, "wa_s")
+        wb_raw = [rt([P, PACK, H], F32, "wb_raw0", 14400), rt([P, PACK, H], F32, "wb_raw1", 22592)]
         wb_bf = [kt([P, PACK * H], BF16, "wb_bf%d" % a) for a in range(2)]
         wb_w = [kt([P, H], U32, "wb_w%d" % a) for a in range(2)]
         wb_s = [kt([P, H], U8, "wb_s%d" % a) for a in range(2)]
-        ua_raw = [rt([P, PACK, 2 * P], F32, "ua_raw0", 64)]
-        ua_bf = kt([P, PACK * N], BF16, "ua_bf")
+        ua_raw = [rt([P, PACK, 2 * P], F32, "ua_raw0", 64), rt([P, PACK, 2 * P], F32, "ua_raw1", 14400)]
+        ua_bf = [kt([P, 2 * KP], BF16, "ua_bf0"), rt([P, 2 * KP], BF16, "ua_bf1", 34816)]
         ua_w = kt([P, N], U32, "ua_w")
         ua_s = kt([P, N], U8, "ua_s")
         ub_w = rt([P, N], I32, "ub_w", 4160)
-        ub_s = rt([P, N], U8, "ub_s", 11328)
+        ub_s = kt([P, N], U8, "ub_s")
         wgt = rt([P, S], F32, "wgt", 6208)
-        h_bf = [[rt([P, PACK * SP], BF16, "h_bf01", 24128) if (b, s) == (0, 1) else
-                 kt([P, PACK * SP], BF16, "h_bf%d%d" % (b, s)) for s in range(S // SP)] for b in range(2)]
+        h_in = [[kt([P, PACK * SP], BF16, "h_a0"), rt([P, PACK * SP], BF16, "h_a1", 18496),
+                 rt([P, PACK * 2 * SP], BF16, "h_a2", -2048)],
+                [rt([P, PACK * SP], BF16, "h_b0", 2048), rt([P, PACK * SP], BF16, "h_b1", 40960),
+                 rt([P, PACK * 2 * SP], BF16, "h_b2", 30784)]]
         h_w = [kt([P, S], U32, "h_w%d" % b) for b in range(2)]
         h_s = [kt([P, S], U8, "h_s%d" % b) for b in range(2)]
-        page = [kt([P, T2], F32, "page0"), rt([P, T2], F32, "page1", 11840)]
+        page = [kt([P, T2], F32, "page0"), kt([P, T2], F32, "page1")]
+        y_whole = [kt([P, S], F32, "y%d" % nt) for nt in (0, 2, 3)]
+        y_one = [rt([P, SP], F32, "y1_0", 40960), rt([P, SP], F32, "y1_1", 33856), rt([P, 2 * SP], F32, "y1_2", 34880)]
 
-        for q in range(4):
-            nc.vector.memset(tabs[32 * q:32 * q + 24, :].bitcast(I32), 0)
-        nc.gpsimd.memset(was_raw[:].rearrange("p a c -> p (a c)").bitcast(I32), 0)
-        for q in range(4):
-            nc.scalar.dma_start(was_raw[32 * q:32 * q + 4, :, :].bitcast(I32),
-                                wa4_scales[:, 4 * q:4 * q + 4, :].rearrange("a r c -> r a c").bitcast(I32))
-        nc.gpsimd.memset(vs[96:P, :, :].rearrange("p a j -> p (a j)").bitcast(I32), 0)
+        def y(nt, j0, j1):
+            if nt == 1:
+                return y_one[j0 // SP][:]
+            return y_whole[max(nt - 1, 0)][:, j0:j1]
+
+        nc.gpsimd.memset(ub_s[:].bitcast(I32), 0)
+        nc.gpsimd.memset(wa_s[:].rearrange("p a c -> p (a c)").bitcast(I32), 0)
+        for p0, p1 in ((0, 16), (32, 48), (64, 128)):
+            nc.vector.memset(tabs[p0:p1, :].bitcast(I32), 0)
+        for i in range(2):
+            nc.vector.memset(page[i][:], 0.0)
 
         def load_words(a):
             nc.sync.dma_start(tabw[a][:], tab_words[a].rearrange("p t i -> p (t i)").bitcast(I32))
 
-        def load_wb(dst, a):
-            nc.sync.dma_start(dst[:], wb[a * KP:(a + 1) * KP, :].rearrange("(p j) c -> p j c", j=PACK))
+        def load_wb(a, c0, c1):
+            nc.sync.dma_start(wb_raw[a][:, :, c0:c1],
+                              wb[a * KP:(a + 1) * KP, c0:c1].rearrange("(p j) c -> p j c", j=PACK))
 
         def load_ua(h):
             rows = ua.rearrange("(g t i) n -> t g i n", t=PACK, i=8)
@@ -90,167 +96,209 @@ def tile_list_twin_critic_replay_kernel(tc, tab_words, tab_scales, offs, wa4_wor
                 nc.sync.dma_start(ua_raw[h][:, t, :], rows[t][:, :, h * 2 * P:(h + 1) * 2 * P])
 
         nc.sync.dma_start(idx[:], offs)
+        scale_rows = tab_scales.rearrange("a (h q r) t -> q (a h) r t", h=2, q=2)
+        for q in range(2):
+            nc.sync.dma_start(tabs[32 * q + 16:32 * q + 32, :].bitcast(I32), scale_rows[q].bitcast(I32))
         for q in range(4):
-            nc.sync.dma_start(tabs[32 * q + 24:32 * q + 32, :].bitcast(I32), tab_scales[:, 4 * q:4 * q + 4, :].bitcast(I32))
+            nc.sync.dma_start(was_raw[32 * q:32 * q + 4, :, :].bitcast(I32),
+                              wa4_scales[:, 4 * q:4 * q + 4, :].rearrange("a r c -> r a c").bitcast(I32))
         load_words(0)
-        load_wb(wb_first, 0)
+        for q in range(4):
+            nc.sync.dma_start(ub_s[32 * q:32 * q + 4, :].bitcast(I32), ub8_scales[0, 4 * q:4 * q + 4, :].bitcast(I32))
         nc.sync.dma_start(wa_raw[:].bitcast(I32), wa4_words.rearrange("a p c -> p a c").bitcast(I32))
         load_words(1)
         nc.sync.dma_start(idx2[:], offs2)
 
-        def gather_words(dst, a, j0, j1):
-            nc.vector.tensor_copy(dst, tabw[a][:].bitcast(U32).indirect(idx[:, j0 // 16:j1 // 16]))
+        def gather_words(a, j0, j1):
+            nc.vector.tensor_copy(vw[a][:, j0:j1], tabw[a][:].bitcast(U32).indirect(idx[:, j0 // 16:j1 // 16]))
 
-        def cast_wb(a, raw, c0, c1, on_vector=False):
+        def reorder(put, raw, words):
+            nc.vector.tensor_copy(put.bitcast(I32).rearrange("p a (t g i) -> p a g t i", t=PACK, i=words),
+                                  raw.bitcast(I32).rearrange("p a (g t i) -> p a g t i", t=PACK, i=words))
+
+        def cast_wb(a, c0, c1, on_vector=False):
             dst = wb_bf[a][:].rearrange("p (t m j) -> p m t j", t=PACK, j=PACK)[:, c0 // PACK:c1 // PACK, :, :]
-            src = raw.rearrange("p j (m t) -> p m t j", t=PACK)
+            src = wb_raw[a][:, :, c0:c1].rearrange("p j (m t) -> p m t j", t=PACK)
             if on_vector:
                 nc.vector.tensor_copy(dst, src)
             else:
                 nc.scalar.activation(dst, src, ACT.Copy)
 
+        def bank_tile(k):
+            return psum.tile([P, 512], F32, name="bank%d" % k)
+
         def quant_wb(a, c0, c1):
             nc.vector.quantize_mx(out=wb_w[a][:, c0:c1].bitcast(FP8X4), scales=wb_s[a][:, c0:c1],
                                   in_=wb_bf[a][:, PACK * c0:PACK * c1])
 
-        def cast_ua(nt):
-            raw = ua_raw[nt // 2][:, :, (nt % 2) * P:(nt % 2 + 1) * P]
-            dst = ua_bf[:, nt * KP:(nt + 1) * KP].rearrange("p (c i j) -> p c j i", i=4, j=PACK)
-            nc.scalar.activation(dst, raw.rearrange("p j (c i) -> p c j i", i=4), ACT.Copy)
+        def cast_ua(h, c0, c1, on_vector=False):
+            dst = ua_bf[h][:, PACK * c0:PACK * c1].rearrange("p (c i j) -> p c j i", i=4, j=PACK)
+            src = ua_raw[h][:, :, c0:c1].rearrange("p j (c i) -> p c j i", i=4)
+            if on_vector:
+                nc.vector.tensor_copy(dst, src)
+            else:
+                nc.scalar.activation(dst, src, ACT.Copy)
 
         def quant_ua(n0, n1):
             cols = slice(n0 * P, n1 * P)
             nc.vector.quantize_mx(out=ua_w[:, cols].bitcast(FP8X4), scales=ua_s[:, cols],
-                                  in_=ua_bf[:, n0 * KP:n1 * KP])
-
-        def table_words(a, jb):
-            if a == 0:
-                return vw0[:, jb * JB:(jb + 1) * JB]
-            piece = min(jb // 2, 2)
-            j0 = jb * JB - piece * SP
-            return vw1[piece][:, j0:j0 + JB]
+                                  in_=ua_bf[n0 // 2][:, n0 % 2 * KP:(n0 % 2 + n1 - n0) * KP])
 
         def one_pass(b, jb, bank, a, t):
             cols = slice(t * P, (t + 1) * P)
+            js = slice(jb * JB, (jb + 1) * JB)
             if b == 0:
                 lhs = wa_w[:, a, 2 * t * P:2 * (t + 1) * P].bitcast(FP4X4)
                 lhs_s = wa_s[:, a, cols]
             else:
                 lhs = wb_w[a][:, cols].bitcast(FP8X4)
                 lhs_s = wb_s[a][:, cols]
-            nc.tensor.matmul_mx(out=bank[:, t, :], lhsT=lhs, lhsT_scale=lhs_s, rhs=table_words(a, jb).bitcast(FP8X4),
-                                rhs_scale=vs[:, a, jb * JB:(jb + 1) * JB],
+            nc.tensor.matmul_mx(out=bank[:, cols], lhsT=lhs, lhsT_scale=lhs_s, rhs=vw[a][:, js].bitcast(FP8X4),
+                                rhs_scale=vs[:, a, js],
                                 start=(a == 0 and t == 0), stop=(a == 1 and t == PACK - 1))
 
+        def h_bf(b, j0, j1):
+            s = min(j0 // SP, 2)
+            return h_in[b][s][:, PACK * (j0 - s * SP):PACK * (j1 - s * SP)]
+
         def relu(b, jb, bank, on_vector=False):
-            off = (jb % 2) * KP
-            dst = h_bf[b][jb // 2][:, off:off + KP].rearrange("p (n t) -> p n t", t=PACK)
-            src = bank[:].rearrange("p t n -> p n t")
+            dst = h_bf(b, jb * JB, (jb + 1) * JB).rearrange("p (n t) -> p n t", t=PACK)
+            src = bank[:].rearrange("p (t n) -> p n t", t=PACK)
             if on_vector:
                 nc.vector.tensor_scalar_max(dst, src, 0.0)
             else:
                 nc.scalar.activation(dst, src, ACT.Relu)
 
-        def hidden(b, jb):
-            bank = ps1.tile([P, PACK, JB], F32, name="bank")
+        def hidden(b, jb, k):
+            bank = bank_tile(k)
             for a in range(2):
                 for t in range(PACK):
                     one_pass(b, jb, bank, a, t)
             relu(b, jb, bank)
 
-        def quant_h(b, s):
-            js = slice(s * SP, (s + 1) * SP)
-            nc.vector.quantize_mx(out=h_w[b][:, js].bitcast(FP8X4), scales=h_s[b][:, js], in_=h_bf[b][s][:])
+        def quant_h(b, j0, j1):
+            nc.vector.quantize_mx(out=h_w[b][:, j0:j1].bitcast(FP8X4), scales=h_s[b][:, j0:j1],
+                                  in_=h_bf(b, j0, j1))
 
-        def span(s):
-            for b in range(2):
-                hidden(b, 2 * s)
-                hidden(b, 2 * s + 1)
-                quant_h(b, s)
-
-        def values(nt, j0, j1, y):
+        def value(b, nt, j0, j1, k):
             cols = slice(nt * P, (nt + 1) * P)
-            n = j1 - j0
-            ya = ps2.tile([P, 512], F32, name="ya")
-            yb = ps2.tile([P, 512], F32, name="yb")
-            nc.tensor.matmul_mx(out=ya[:, 0:n], lhsT=ua_w[:, cols].bitcast(FP8X4), lhsT_scale=ua_s[:, cols],
-                                rhs=h_w[0][:, j0:j1].bitcast(FP8X4), rhs_scale=h_s[0][:, j0:j1], start=True, stop=True)
-            nc.tensor.matmul_mx(out=yb[:, 0:n], lhsT=ub_w[:, cols].bitcast(FP8X4), lhsT_scale=ub_s[:, cols],
-                                rhs=h_w[1][:, j0:j1].bitcast(FP8X4), rhs_scale=h_s[1][:, j0:j1], start=True, stop=True)
-            ya_sb = ring.tile([P, 512], F32, name="ya_sb")
-            nc.scalar.copy(ya_sb[:, 0:n], ya[:, 0:n])
-            nc.vector.tensor_tensor(y, yb[:, 0:n], ya_sb[:, 0:n], ALU.min)
+            bank = bank_tile(k)
+            u_w, u_s = ((ua_w, ua_s), (ub_w, ub_s))[b]
+            nc.tensor.matmul_mx(out=bank[:, 0:j1 - j0], lhsT=u_w[:, cols].bitcast(FP8X4), lhsT_scale=u_s[:, cols],
+                                rhs=h_w[b][:, j0:j1].bitcast(FP8X4), rhs_scale=h_s[b][:, j0:j1], start=True, stop=True)
+            return bank[:, 0:j1 - j0]
 
-        def scatter(nt, j0, j1, y):
-            nc.vector.tensor_tensor(page[nt % 2][:].indirect(idx2[:, j0 // 16:j1 // 16]), y, wgt[:, j0:j1], ALU.mult)
+        def value_a(nt, j0, j1, k):
+            ya = value(0, nt, j0, j1, k)
+            ya_sb = ring.tile([P, 512], F32, name="ya_sb")
+            nc.scalar.copy(ya_sb[:, 0:j1 - j0], ya)
+            return ya_sb[:, 0:j1 - j0]
+
+        def minimum(nt, j0, j1, ya_sb, k):
+            nc.vector.tensor_tensor(y(nt, j0, j1), value(1, nt, j0, j1, k), ya_sb, ALU.min)
+
+        def values(nt, j0, j1, k):
+            minimum(nt, j0, j1, value_a(nt, j0, j1, k), k + 1)
+
+        def scatter(nt, j0, j1):
+            nc.vector.tensor_tensor(page[nt % 2][:].indirect(idx2[:, j0 // 16:j1 // 16]), y(nt, j0, j1),
+                                    wgt[:, j0:j1], ALU.mult)
 
         def store(nt):
             nc.sync.dma_start(out[nt * P:(nt + 1) * P, :], page[nt % 2][:])
 
         nc.vector.tensor_copy(vs_top[:], tabs[:].indirect(idx[:]))
         for a in range(2):
-            nc.sync.dma_start(vs[0:100, a, :].bitcast(I32), vs_top[24 + 4 * a:124 + 4 * a, :].bitcast(I32))
-        load_wb(wb_last, 1)
-        gather_words(vw0[:], 0, 0, S)
-        nc.vector.memset(ub_s[:].bitcast(I32), 0)
-        for i in range(2):
-            for c in range(0, T2, 512):
-                nc.vector.memset(page[i][:, c:c + 512], 0.0)
+            for h in range(2):
+                p0 = 16 + 8 * a + 4 * h
+                nc.sync.dma_start(vs[64 * h:64 * h + 64, a, :].bitcast(I32), vs_top[p0:p0 + 64, :].bitcast(I32))
+        load_wb(0, 0, H)
+        load_wb(1, 0, H // 2)
+        load_wb(1, H // 2, H)
+        for q in range(4):
+            reorder(wa_s[32 * q:32 * q + 4, :, :], was_raw[32 * q:32 * q + 4, :, :], 2)
+        gather_words(0, 0, S)
         load_ua(0)
         nc.sync.dma_start(ub_w[:], ub8_words[0].rearrange("p c i -> p (c i)").bitcast(I32))
-        for q in range(4):
-            nc.sync.dma_start(ub_s[32 * q:32 * q + 4, :].bitcast(I32), ub8_scales[0, 4 * q:4 * q + 4, :].bitcast(I32))
         nc.sync.dma_start(wgt[:], wgo)
-        cast_wb(0, wb_first[:], 0, H)
-        ua_raw.append(kt([P, PACK, 2 * P], F32, "wb_first"))
+        reorder(wa_w[:], wa_raw[:], 4)
+        gather_words(1, 0, SP)
+        gather_words(1, SP, S)
+        banks_a = [bank_tile(2 + jb) for jb in range(6)]
+        for jb in range(4):
+            for a in range(2):
+                for t in range(PACK):
+                    one_pass(0, jb, banks_a[jb], a, t)
+        relu(0, 0, banks_a[0])
+        relu(0, 1, banks_a[1])
+        cast_wb(0, 0, CUT)
+        cast_wb(0, CUT, H, True)
         load_ua(1)
-        for raw, put, words in ((wa_raw, wa_w, 4), (was_raw, wa_s, 2)):
-            nc.vector.tensor_copy(put[:].bitcast(I32).rearrange("p a (t g i) -> p a g t i", t=PACK, i=words),
-                                  raw[:].bitcast(I32).rearrange("p a (g t i) -> p a g t i", t=PACK, i=words))
-        gather_words(vw1[0][:], 1, 0, SP)
         quant_wb(0, 0, H)
-        gather_words(vw1[1][:], 1, SP, 2 * SP)
-        hidden(0, 0)
-        hidden(0, 1)
-        quant_h(0, 0)
-        cast_wb(1, wb_last[:, :, 0:CUT], 0, CUT)
-        cast_wb(1, wb_last[:, :, CUT:H], CUT, H, True)
+        banks = [bank_tile(jb) for jb in range(2)]
+        for t in range(PACK):
+            for jb in range(2):
+                one_pass(1, jb, banks[jb], 0, t)
+        for jb in range(4, 6):
+            for a in range(2):
+                for t in range(PACK):
+                    one_pass(0, jb, banks_a[jb], a, t)
+        cast_wb(1, 0, H // 2)
+        cast_wb(1, H // 2, H, True)
         quant_wb(1, 0, H // 2)
         quant_wb(1, H // 2, H)
-        banks = [ps1.tile([P, PACK, JB], F32, name="bank") for jb in range(2)]
-        for a in range(2):
-            for t in range(PACK):
-                for jb in range(2):
-                    one_pass(1, jb, banks[jb], a, t)
-        cast_ua(0)
+        for t in range(PACK):
+            for jb in range(2):
+                one_pass(1, jb, banks[jb], 1, t)
+        quant_h(0, 0, SP)
+        relu(0, 2, banks_a[2])
+        relu(0, 3, banks_a[3])
+        quant_h(0, SP, 2 * SP)
+        cast_ua(0, 0, P, True)
+        cast_ua(0, P, 2 * P)
         quant_ua(0, 1)
+        ya0 = value_a(0, 0, SP, 2)
         relu(1, 0, banks[0])
         relu(1, 1, banks[1], True)
-        quant_h(1, 0)
-        vw1.append(kt([P, 2 * SP], U32, "h_bf10"))
-        gather_words(vw1[2][:], 1, 2 * SP, S)
-        for s in range(3):
-            y = ring.tile([P, S], F32, name="y")
-            values(0, s * SP, (s + 1) * SP, y[:, 0:SP])
-            scatter(0, s * SP, (s + 1) * SP, y[:, 0:SP])
-            if s == 0:
-                cast_ua(1)
-                quant_ua(1, 2)
-            span(s + 1)
-            y = kt([P, SP], F32, "h_bf1%d" % (s + 1))
-            values(1, s * SP, (s + 1) * SP, y[:])
-            scatter(1, s * SP, (s + 1) * SP, y[:])
-        for nt in range(2):
-            y = ring.tile([P, S], F32, name="y")
-            values(nt, 3 * SP, S, y[:, 0:SP])
-            scatter(nt, 3 * SP, S, y[:, 0:SP])
-            store(nt)
-        cast_ua(2)
-        cast_ua(3)
+        quant_h(1, 0, SP)
+        minimum(0, 0, SP, ya0, 3)
+        quant_ua(1, 2)
+        ya1 = value_a(1, 0, SP, 4)
+        scatter(0, 0, SP)
+        hidden(1, 2, 0)
+        hidden(1, 3, 1)
+        quant_h(1, SP, 2 * SP)
+        minimum(1, 0, SP, ya1, 5)
+        scatter(1, 0, SP)
+        values(0, SP, 2 * SP, 2)
+        ya1 = value_a(1, SP, 2 * SP, 4)
+        relu(0, 4, banks_a[4])
+        relu(0, 5, banks_a[5])
+        scatter(0, SP, 2 * SP)
+        hidden(0, 6, 6)
+        hidden(0, 7, 7)
+        quant_h(0, 2 * SP, S)
+        hidden(1, 4, 0)
+        hidden(1, 5, 1)
+        hidden(1, 6, 6)
+        hidden(1, 7, 7)
+        quant_h(1, 2 * SP, S)
+        minimum(1, SP, 2 * SP, ya1, 5)
+        scatter(1, SP, 2 * SP)
+        values(0, 2 * SP, S, 2)
+        ya1 = value_a(1, 2 * SP, S, 4)
+        scatter(0, 2 * SP, S)
+        store(0)
+        cast_ua(1, 0, 2 * P)
         quant_ua(2, 4)
-        for nt in range(2, N // P):
-            y = ring.tile([P, S], F32, name="y")
-            for j0 in (0, 512):
-                values(nt, j0, j0 + 512, y[:, j0:j0 + 512])
-            scatter(nt, 0, S, y[:])
-            store(nt)
+        minimum(1, 2 * SP, S, ya1, 5)
+        scatter(1, 2 * SP, S)
+        store(1)
+        values(2, 0, 512, 0)
+        values(2, 512, S, 6)
+        values(3, 0, 512, 2)
+        scatter(2, 0, S)
+        store(2)
+        values(3, 512, S, 4)
+        scatter(3, 0, S)
+        store(3)

@@ -49,27 +49,27 @@ def tile_list_twin_critic_replay_kernel(tc, tab_words, tab_scales, offs, wa4_wor
         wa_raw = kt([P, 2, 2 * H], U8, "wa_raw")
         wa_w = kt([P, 2, 2 * H], U8, "wa_w")
         was_raw = kt([P, 2, H], U8, "was_raw")
-        wa_s = kt([P, 2, H], U8, "wa_s")
+        wa_s = rt([P, 2, H], U8, "wa_s", 10880)
         wb_raw = [rt([P, PACK, H], F32, "wb_raw0", 14400), rt([P, PACK, H], F32, "wb_raw1", 22592)]
         wb_bf = [kt([P, PACK * H], BF16, "wb_bf%d" % a) for a in range(2)]
         wb_w = [kt([P, H], U32, "wb_w%d" % a) for a in range(2)]
         wb_s = [kt([P, H], U8, "wb_s%d" % a) for a in range(2)]
-        ua_raw = [rt([P, PACK, 2 * P], F32, "ua_raw0", 64), rt([P, PACK, 2 * P], F32, "ua_raw1", 14400)]
-        ua_bf = [kt([P, 2 * KP], BF16, "ua_bf0"), rt([P, 2 * KP], BF16, "ua_bf1", 34816)]
+        ua_raw = [rt([P, PACK, 2 * P], F32, "ua_raw0", 64), rt([P, PACK, 2 * P], F32, "ua_raw1", 39040)]
+        ua_bf = [kt([P, 2 * KP], BF16, "ua_bf0"), rt([P, 2 * KP], BF16, "ua_bf1", -3968)]
         ua_w = kt([P, N], U32, "ua_w")
         ua_s = kt([P, N], U8, "ua_s")
-        ub_w = rt([P, N], I32, "ub_w", 4160)
+        ub_w = rt([P, N], I32, "ub_w", 4224)
         ub_s = kt([P, N], U8, "ub_s")
-        wgt = rt([P, S], F32, "wgt", 6208)
-        h_in = [[kt([P, PACK * SP], BF16, "h_a0"), rt([P, PACK * SP], BF16, "h_a1", 18496),
-                 rt([P, PACK * 2 * SP], BF16, "h_a2", -2048)],
-                [rt([P, PACK * SP], BF16, "h_b0", 2048), rt([P, PACK * SP], BF16, "h_b1", 40960),
-                 rt([P, PACK * 2 * SP], BF16, "h_b2", 30784)]]
+        wgt = rt([P, S], F32, "wgt", 6272)
+        h_in = [[rt([P, PACK * SP], BF16, "h_a0", 39040), rt([P, PACK * SP], BF16, "h_a1", 20096),
+                 rt([P, PACK * 2 * SP], BF16, "h_a2", -3968)],
+                [rt([P, PACK * SP], BF16, "h_b0", 128), rt([P, PACK * SP], BF16, "h_b1", 2176),
+                 kt([P, PACK * 2 * SP], BF16, "h_b2")]]
         h_w = [kt([P, S], U32, "h_w%d" % b) for b in range(2)]
         h_s = [kt([P, S], U8, "h_s%d" % b) for b in range(2)]
-        page = [kt([P, T2], F32, "page0"), kt([P, T2], F32, "page1")]
+        page = [kt([P, T2], F32, "page0"), rt([P, T2], F32, "page1", 11904)]
         y_whole = [kt([P, S], F32, "y%d" % nt) for nt in (0, 2, 3)]
-        y_one = [rt([P, SP], F32, "y1_0", 40960), rt([P, SP], F32, "y1_1", 33856), rt([P, 2 * SP], F32, "y1_2", 34880)]
+        y_one = [rt([P, SP], F32, "y1_0", 2176), rt([P, SP], F32, "y1_1", -1920), kt([P, 2 * SP], F32, "y1_2")]
 
         def y(nt, j0, j1):
             if nt == 1:
@@ -77,11 +77,10 @@ def tile_list_twin_critic_replay_kernel(tc, tab_words, tab_scales, offs, wa4_wor
             return y_whole[max(nt - 1, 0)][:, j0:j1]
 
         nc.gpsimd.memset(ub_s[:].bitcast(I32), 0)
-        nc.gpsimd.memset(wa_s[:].rearrange("p a c -> p (a c)").bitcast(I32), 0)
+        nc.gpsimd.memset(was_raw[:].rearrange("p a c -> p (a c)").bitcast(I32), 0)
         for p0, p1 in ((0, 16), (32, 48), (64, 128)):
-            nc.vector.memset(tabs[p0:p1, :].bitcast(I32), 0)
-        for i in range(2):
-            nc.vector.memset(page[i][:], 0.0)
+            nc.gpsimd.memset(tabs[p0:p1, :].bitcast(I32), 0)
+        nc.vector.memset(page[0][:], 0.0)
 
         def load_words(a):
             nc.sync.dma_start(tabw[a][:], tab_words[a].rearrange("p t i -> p (t i)").bitcast(I32))
@@ -100,11 +99,11 @@ def tile_list_twin_critic_replay_kernel(tc, tab_words, tab_scales, offs, wa4_wor
         for q in range(2):
             nc.sync.dma_start(tabs[32 * q + 16:32 * q + 32, :].bitcast(I32), scale_rows[q].bitcast(I32))
         for q in range(4):
-            nc.sync.dma_start(was_raw[32 * q:32 * q + 4, :, :].bitcast(I32),
-                              wa4_scales[:, 4 * q:4 * q + 4, :].rearrange("a r c -> r a c").bitcast(I32))
+            nc.sync.dma_start(ub_s[32 * q:32 * q + 4, :].bitcast(I32), ub8_scales[0, 4 * q:4 * q + 4, :].bitcast(I32))
         load_words(0)
         for q in range(4):
-            nc.sync.dma_start(ub_s[32 * q:32 * q + 4, :].bitcast(I32), ub8_scales[0, 4 * q:4 * q + 4, :].bitcast(I32))
+            nc.sync.dma_start(was_raw[32 * q:32 * q + 4, :, :].bitcast(I32),
+                              wa4_scales[:, 4 * q:4 * q + 4, :].rearrange("a r c -> r a c").bitcast(I32))
         nc.sync.dma_start(wa_raw[:].bitcast(I32), wa4_words.rearrange("a p c -> p a c").bitcast(I32))
         load_words(1)
         nc.sync.dma_start(idx2[:], offs2)
@@ -213,18 +212,16 @@ def tile_list_twin_critic_replay_kernel(tc, tab_words, tab_scales, offs, wa4_wor
                 p0 = 16 + 8 * a + 4 * h
                 nc.sync.dma_start(vs[64 * h:64 * h + 64, a, :].bitcast(I32), vs_top[p0:p0 + 64, :].bitcast(I32))
         load_wb(0, 0, H)
-        load_wb(1, 0, H // 2)
-        load_wb(1, H // 2, H)
-        for q in range(4):
-            reorder(wa_s[32 * q:32 * q + 4, :, :], was_raw[32 * q:32 * q + 4, :, :], 2)
+        load_wb(1, 0, H)
         gather_words(0, 0, S)
         load_ua(0)
         nc.sync.dma_start(ub_w[:], ub8_words[0].rearrange("p c i -> p (c i)").bitcast(I32))
         nc.sync.dma_start(wgt[:], wgo)
         reorder(wa_w[:], wa_raw[:], 4)
+        reorder(wa_s[:], was_raw[:], 2)
         gather_words(1, 0, SP)
         gather_words(1, SP, S)
-        banks_a = [bank_tile(2 + jb) for jb in range(6)]
+        banks_a = [bank_tile(2 + jb) for jb in range(4)]
         for jb in range(4):
             for a in range(2):
                 for t in range(PACK):
@@ -233,24 +230,21 @@ def tile_list_twin_critic_replay_kernel(tc, tab_words, tab_scales, offs, wa4_wor
         relu(0, 1, banks_a[1])
         cast_wb(0, 0, CUT)
         cast_wb(0, CUT, H, True)
-        load_ua(1)
         quant_wb(0, 0, H)
-        banks = [bank_tile(jb) for jb in range(2)]
-        for t in range(PACK):
-            for jb in range(2):
+        nc.vector.memset(page[1][:], 0.0)
+        banks = [bank_tile(k) for k in (0, 1, 6, 7)]
+        for jb in range(4):
+            for t in range(PACK):
                 one_pass(1, jb, banks[jb], 0, t)
-        for jb in range(4, 6):
-            for a in range(2):
-                for t in range(PACK):
-                    one_pass(0, jb, banks_a[jb], a, t)
-        cast_wb(1, 0, H // 2)
-        cast_wb(1, H // 2, H, True)
+        cast_wb(1, 0, CUT)
+        cast_wb(1, CUT, H, True)
         quant_wb(1, 0, H // 2)
         quant_wb(1, H // 2, H)
         for t in range(PACK):
             for jb in range(2):
                 one_pass(1, jb, banks[jb], 1, t)
         quant_h(0, 0, SP)
+        load_ua(1)
         relu(0, 2, banks_a[2])
         relu(0, 3, banks_a[3])
         quant_h(0, SP, 2 * SP)
@@ -265,40 +259,41 @@ def tile_list_twin_critic_replay_kernel(tc, tab_words, tab_scales, offs, wa4_wor
         quant_ua(1, 2)
         ya1 = value_a(1, 0, SP, 4)
         scatter(0, 0, SP)
-        hidden(1, 2, 0)
-        hidden(1, 3, 1)
+        for jb in range(2, 4):
+            for t in range(PACK):
+                one_pass(1, jb, banks[jb], 1, t)
+            relu(1, jb, banks[jb])
         quant_h(1, SP, 2 * SP)
         minimum(1, 0, SP, ya1, 5)
         scatter(1, 0, SP)
         values(0, SP, 2 * SP, 2)
         ya1 = value_a(1, SP, 2 * SP, 4)
-        relu(0, 4, banks_a[4])
-        relu(0, 5, banks_a[5])
         scatter(0, SP, 2 * SP)
-        hidden(0, 6, 6)
-        hidden(0, 7, 7)
-        quant_h(0, 2 * SP, S)
         hidden(1, 4, 0)
         hidden(1, 5, 1)
         hidden(1, 6, 6)
         hidden(1, 7, 7)
         quant_h(1, 2 * SP, S)
+        hidden(0, 4, 0)
+        hidden(0, 5, 1)
+        hidden(0, 6, 6)
+        hidden(0, 7, 7)
+        quant_h(0, 2 * SP, S)
         minimum(1, SP, 2 * SP, ya1, 5)
         scatter(1, SP, 2 * SP)
-        values(0, 2 * SP, S, 2)
-        ya1 = value_a(1, 2 * SP, S, 4)
-        scatter(0, 2 * SP, S)
-        store(0)
         cast_ua(1, 0, 2 * P)
         quant_ua(2, 4)
-        minimum(1, 2 * SP, S, ya1, 5)
+        values(0, 2 * SP, S, 2)
+        values(1, 2 * SP, S, 4)
+        scatter(0, 2 * SP, S)
+        store(0)
+        values(2, 0, 512, 6)
+        values(2, 512, S, 0)
         scatter(1, 2 * SP, S)
         store(1)
-        values(2, 0, 512, 0)
-        values(2, 512, S, 6)
         values(3, 0, 512, 2)
+        values(3, 512, S, 4)
         scatter(2, 0, S)
         store(2)
-        values(3, 512, S, 4)
         scatter(3, 0, S)
         store(3)

@@ -41,35 +41,35 @@ def tile_list_twin_critic_replay_kernel(tc, tab_words, tab_scales, offs, wa4_wor
 
         idx = keep.tile([P, S // 16], U16, name="idx")
         idx2 = keep.tile([P, S // 16], U16, name="idx2")
-        tabw = [rt([P, T], I32, "tabw0", 4096), kt([P, T], I32, "tabw1")]
+        tabw = [rt([P, T], I32, "tabw0", 4096), rt([P, T], I32, "tabw1", 30784)]
         tabs = rt([P, T], U8, "tabs", 22528)
         vw = [kt([P, S], U32, "vw%d" % a) for a in range(2)]
         vs_top = kt([P, S], U8, "vs_top")
         vs = kt([P, 2, S], U8, "vs")
         wa_raw = kt([P, 2, 2 * H], U8, "wa_raw")
         wa_w = kt([P, 2, 2 * H], U8, "wa_w")
-        was_raw = kt([P, 2, H], U8, "was_raw")
+        was_raw = rt([P, 2, H], U8, "was_raw", 43136)
         wa_s = rt([P, 2, H], U8, "wa_s", 10880)
         wb_raw = [rt([P, PACK, H], F32, "wb_raw0", 14400), rt([P, PACK, H], F32, "wb_raw1", 22592)]
         wb_bf = [kt([P, PACK * H], BF16, "wb_bf%d" % a) for a in range(2)]
         wb_w = [kt([P, H], U32, "wb_w%d" % a) for a in range(2)]
         wb_s = [kt([P, H], U8, "wb_s%d" % a) for a in range(2)]
-        ua_raw = [rt([P, PACK, 2 * P], F32, "ua_raw0", 64), rt([P, PACK, 2 * P], F32, "ua_raw1", 39040)]
+        ua_raw = [rt([P, PACK, 2 * P], F32, "ua_raw0", 64), rt([P, PACK, 2 * P], F32, "ua_raw1", 14400)]
         ua_bf = [kt([P, 2 * KP], BF16, "ua_bf0"), rt([P, 2 * KP], BF16, "ua_bf1", -3968)]
         ua_w = kt([P, N], U32, "ua_w")
         ua_s = kt([P, N], U8, "ua_s")
-        ub_w = rt([P, N], I32, "ub_w", 4224)
+        ub_w = rt([P, N], I32, "ub_w", 41152)
         ub_s = kt([P, N], U8, "ub_s")
-        wgt = rt([P, S], F32, "wgt", 6272)
-        h_in = [[rt([P, PACK * SP], BF16, "h_a0", 39040), rt([P, PACK * SP], BF16, "h_a1", 20096),
+        wgt = rt([P, S], F32, "wgt", 43200)
+        h_in = [[kt([P, PACK * SP], BF16, "h_a0"), rt([P, PACK * SP], BF16, "h_a1", 22592),
                  rt([P, PACK * 2 * SP], BF16, "h_a2", -3968)],
-                [rt([P, PACK * SP], BF16, "h_b0", 128), rt([P, PACK * SP], BF16, "h_b1", 2176),
+                [rt([P, PACK * SP], BF16, "h_b0", 47296), rt([P, PACK * SP], BF16, "h_b1", 47360),
                  kt([P, PACK * 2 * SP], BF16, "h_b2")]]
-        h_w = [kt([P, S], U32, "h_w%d" % b) for b in range(2)]
+        h_w = [rt([P, S], U32, "h_w0", 24640), kt([P, S], U32, "h_w1")]
         h_s = [kt([P, S], U8, "h_s%d" % b) for b in range(2)]
-        page = [kt([P, T2], F32, "page0"), rt([P, T2], F32, "page1", 11904)]
+        page = [kt([P, T2], F32, "page0"), rt([P, T2], F32, "page1", 30784)]
         y_whole = [kt([P, S], F32, "y%d" % nt) for nt in (0, 2, 3)]
-        y_one = [rt([P, SP], F32, "y1_0", 2176), rt([P, SP], F32, "y1_1", -1920), kt([P, 2 * SP], F32, "y1_2")]
+        y_one = [rt([P, SP], F32, "y1_0", 47424), rt([P, SP], F32, "y1_1", -1920), kt([P, 2 * SP], F32, "y1_2")]
 
         def y(nt, j0, j1):
             if nt == 1:
@@ -221,17 +221,18 @@ def tile_list_twin_critic_replay_kernel(tc, tab_words, tab_scales, offs, wa4_wor
         reorder(wa_s[:], was_raw[:], 2)
         gather_words(1, 0, SP)
         gather_words(1, SP, S)
-        banks_a = [bank_tile(2 + jb) for jb in range(4)]
-        for jb in range(4):
+        nc.vector.memset(page[1][:], 0.0)
+        hidden(0, 0, 2)
+        hidden(0, 1, 3)
+        banks_a = [bank_tile(2 + jb) for jb in range(2)]
+        for jb in range(2):
             for a in range(2):
                 for t in range(PACK):
-                    one_pass(0, jb, banks_a[jb], a, t)
-        relu(0, 0, banks_a[0])
-        relu(0, 1, banks_a[1])
-        cast_wb(0, 0, CUT)
-        cast_wb(0, CUT, H, True)
+                    one_pass(0, 2 + jb, banks_a[jb], a, t)
+        cast_wb(0, 0, H // 2)
+        cast_wb(0, H // 2, H, True)
+        load_ua(1)
         quant_wb(0, 0, H)
-        nc.vector.memset(page[1][:], 0.0)
         banks = [bank_tile(k) for k in (0, 1, 6, 7)]
         for jb in range(4):
             for t in range(PACK):
@@ -243,31 +244,30 @@ def tile_list_twin_critic_replay_kernel(tc, tab_words, tab_scales, offs, wa4_wor
         for t in range(PACK):
             for jb in range(2):
                 one_pass(1, jb, banks[jb], 1, t)
-        quant_h(0, 0, SP)
-        load_ua(1)
-        relu(0, 2, banks_a[2])
-        relu(0, 3, banks_a[3])
-        quant_h(0, SP, 2 * SP)
         cast_ua(0, 0, P, True)
-        cast_ua(0, P, 2 * P)
         quant_ua(0, 1)
-        ya0 = value_a(0, 0, SP, 2)
+        quant_h(0, 0, SP)
+        ya0 = value_a(0, 0, SP, 4)
         relu(1, 0, banks[0])
         relu(1, 1, banks[1], True)
         quant_h(1, 0, SP)
-        minimum(0, 0, SP, ya0, 3)
+        minimum(0, 0, SP, ya0, 5)
+        cast_ua(0, P, 2 * P)
         quant_ua(1, 2)
-        ya1 = value_a(1, 0, SP, 4)
+        relu(0, 2, banks_a[0])
+        relu(0, 3, banks_a[1])
+        quant_h(0, SP, 2 * SP)
+        ya1 = value_a(1, 0, SP, 2)
         scatter(0, 0, SP)
         for jb in range(2, 4):
             for t in range(PACK):
                 one_pass(1, jb, banks[jb], 1, t)
             relu(1, jb, banks[jb])
         quant_h(1, SP, 2 * SP)
-        minimum(1, 0, SP, ya1, 5)
+        minimum(1, 0, SP, ya1, 3)
         scatter(1, 0, SP)
-        values(0, SP, 2 * SP, 2)
-        ya1 = value_a(1, SP, 2 * SP, 4)
+        values(0, SP, 2 * SP, 4)
+        ya1 = value_a(1, SP, 2 * SP, 2)
         scatter(0, SP, 2 * SP)
         hidden(1, 4, 0)
         hidden(1, 5, 1)
@@ -279,20 +279,20 @@ def tile_list_twin_critic_replay_kernel(tc, tab_words, tab_scales, offs, wa4_wor
         hidden(0, 6, 6)
         hidden(0, 7, 7)
         quant_h(0, 2 * SP, S)
-        minimum(1, SP, 2 * SP, ya1, 5)
+        minimum(1, SP, 2 * SP, ya1, 3)
         scatter(1, SP, 2 * SP)
         cast_ua(1, 0, 2 * P)
         quant_ua(2, 4)
-        values(0, 2 * SP, S, 2)
-        values(1, 2 * SP, S, 4)
+        values(0, 2 * SP, S, 4)
+        values(1, 2 * SP, S, 2)
         scatter(0, 2 * SP, S)
         store(0)
         values(2, 0, 512, 6)
         values(2, 512, S, 0)
         scatter(1, 2 * SP, S)
         store(1)
-        values(3, 0, 512, 2)
-        values(3, 512, S, 4)
+        values(3, 0, 512, 4)
+        values(3, 512, S, 2)
         scatter(2, 0, S)
         store(2)
         scatter(3, 0, S)

@@ -41,7 +41,7 @@ def tile_list_twin_critic_replay_kernel(tc, tab_words, tab_scales, offs, wa4_wor
 
         idx = keep.tile([P, S // 16], U16, name="idx")
         idx2 = keep.tile([P, S // 16], U16, name="idx2")
-        tabw = [rt([P, T], I32, "tabw0", 4096), rt([P, T], I32, "tabw1", 30784)]
+        tabw = [rt([P, T], I32, "tabw0", 4096), kt([P, T], I32, "tabw1")]
         tabs = rt([P, T], U8, "tabs", 22528)
         vw = [kt([P, S], U32, "vw%d" % a) for a in range(2)]
         vs_top = kt([P, S], U8, "vs_top")
@@ -65,9 +65,9 @@ def tile_list_twin_critic_replay_kernel(tc, tab_words, tab_scales, offs, wa4_wor
                  rt([P, PACK * 2 * SP], BF16, "h_a2", -3968)],
                 [rt([P, PACK * SP], BF16, "h_b0", 47296), rt([P, PACK * SP], BF16, "h_b1", 47360),
                  kt([P, PACK * 2 * SP], BF16, "h_b2")]]
-        h_w = [rt([P, S], U32, "h_w0", 24640), kt([P, S], U32, "h_w1")]
+        h_w = [kt([P, S], U32, "h_w0"), kt([P, S], U32, "h_w1")]
         h_s = [kt([P, S], U8, "h_s%d" % b) for b in range(2)]
-        page = [kt([P, T2], F32, "page0"), rt([P, T2], F32, "page1", 30784)]
+        page = [kt([P, T2], F32, "page0"), kt([P, T2], F32, "page1")]
         y_whole = [kt([P, S], F32, "y%d" % nt) for nt in (0, 2, 3)]
         y_one = [rt([P, SP], F32, "y1_0", 47424), rt([P, SP], F32, "y1_1", -1920), kt([P, 2 * SP], F32, "y1_2")]
 
@@ -80,7 +80,8 @@ def tile_list_twin_critic_replay_kernel(tc, tab_words, tab_scales, offs, wa4_wor
         nc.gpsimd.memset(was_raw[:].rearrange("p a c -> p (a c)").bitcast(I32), 0)
         for p0, p1 in ((0, 16), (32, 48), (64, 128)):
             nc.gpsimd.memset(tabs[p0:p1, :].bitcast(I32), 0)
-        nc.vector.memset(page[0][:], 0.0)
+        for i in range(2):
+            nc.gpsimd.memset(page[i][:], 0.0)
 
         def load_words(a):
             nc.sync.dma_start(tabw[a][:], tab_words[a].rearrange("p t i -> p (t i)").bitcast(I32))
@@ -221,7 +222,6 @@ def tile_list_twin_critic_replay_kernel(tc, tab_words, tab_scales, offs, wa4_wor
         reorder(wa_s[:], was_raw[:], 2)
         gather_words(1, 0, SP)
         gather_words(1, SP, S)
-        nc.vector.memset(page[1][:], 0.0)
         hidden(0, 0, 2)
         hidden(0, 1, 3)
         banks_a = [bank_tile(2 + jb) for jb in range(2)]
@@ -229,8 +229,8 @@ def tile_list_twin_critic_replay_kernel(tc, tab_words, tab_scales, offs, wa4_wor
             for a in range(2):
                 for t in range(PACK):
                     one_pass(0, 2 + jb, banks_a[jb], a, t)
-        cast_wb(0, 0, H // 2)
-        cast_wb(0, H // 2, H, True)
+        cast_wb(0, 0, CUT)
+        cast_wb(0, CUT, H, True)
         load_ua(1)
         quant_wb(0, 0, H)
         banks = [bank_tile(k) for k in (0, 1, 6, 7)]

@@ -21,7 +21,8 @@ PACK = 4
 KP = P * PACK
 JB = 128
 SP = 256
-CUT = 192
+CUT0 = 128
+CUT1 = 160
 
 
 def tile_list_twin_critic_replay_kernel(tc, tab_words, tab_scales, offs, wa4_words, wa4_scales, wb, ua,
@@ -29,7 +30,6 @@ def tile_list_twin_critic_replay_kernel(tc, tab_words, tab_scales, offs, wa4_wor
     nc = tc.nc
     with ExitStack() as ctx:
         keep = ctx.enter_context(tc.tile_pool(name="keep", bufs=1))
-        ring = ctx.enter_context(tc.tile_pool(name="ring", bufs=6))
         reuse = ctx.enter_context(tc.tile_pool(name="reuse", bufs=1))
         psum = ctx.enter_context(tc.psum_pool(name="psum", bufs=1))
 
@@ -37,44 +37,44 @@ def tile_list_twin_critic_replay_kernel(tc, tab_words, tab_scales, offs, wa4_wor
             return keep.tile(shape, dtype, name=name, align_bytes=64)
 
         def rt(shape, dtype, name, offset):
-            return reuse.tile(shape, dtype, name=name, align_bytes=64, offset=4096 + offset)
+            return reuse.tile(shape, dtype, name=name, align_bytes=64, offset=offset)
 
         idx = keep.tile([P, S // 16], U16, name="idx")
         idx2 = keep.tile([P, S // 16], U16, name="idx2")
-        tabw = [rt([P, T], I32, "tabw0", 4096), kt([P, T], I32, "tabw1")]
-        tabs = rt([P, T], U8, "tabs", 22528)
+        tabw = [rt([P, T], I32, "tabw0", 8064), kt([P, T], I32, "tabw1")]
+        tabs = rt([P, T], U8, "tabs", 24448)
         vw = [kt([P, S], U32, "vw%d" % a) for a in range(2)]
         vs_top = kt([P, S], U8, "vs_top")
         vs = kt([P, 2, S], U8, "vs")
-        wa_raw = kt([P, 2, 2 * H], U8, "wa_raw")
-        wa_w = kt([P, 2, 2 * H], U8, "wa_w")
-        was_raw = rt([P, 2, H], U8, "was_raw", 43136)
-        wa_s = rt([P, 2, H], U8, "wa_s", 10880)
-        wb_raw = [rt([P, PACK, H], F32, "wb_raw0", 14400), rt([P, PACK, H], F32, "wb_raw1", 22592)]
+        wa_raw = rt([P, 2, 2 * H], U8, "wa_raw", 34752)
+        wa_w = rt([P, 2, 2 * H], U8, "wa_w", 12288)
+        was_raw = rt([P, 2, H], U8, "was_raw", 41088)
+        wa_s = rt([P, 2, H], U8, "wa_s", 14400)
+        wb_raw = [rt([P, PACK, H], F32, "wb_raw0", 16320), rt([P, PACK, H], F32, "wb_raw1", 24512)]
         wb_bf = [kt([P, PACK * H], BF16, "wb_bf%d" % a) for a in range(2)]
         wb_w = [kt([P, H], U32, "wb_w%d" % a) for a in range(2)]
         wb_s = [kt([P, H], U8, "wb_s%d" % a) for a in range(2)]
-        ua_raw = [rt([P, PACK, 2 * P], F32, "ua_raw0", 64), rt([P, PACK, 2 * P], F32, "ua_raw1", 14400)]
-        ua_bf = [kt([P, 2 * KP], BF16, "ua_bf0"), rt([P, 2 * KP], BF16, "ua_bf1", -3968)]
+        ua_raw = [rt([P, PACK, 2 * P], F32, "ua_raw0", 4096), rt([P, PACK, 2 * P], F32, "ua_raw1", 8128)]
+        ua_bf = [kt([P, 2 * KP], BF16, "ua_bf0"), rt([P, 2 * KP], BF16, "ua_bf1", 38976)]
         ua_w = kt([P, N], U32, "ua_w")
         ua_s = kt([P, N], U8, "ua_s")
-        ub_w = rt([P, N], I32, "ub_w", 41152)
+        ub_w = rt([P, N], I32, "ub_w", 32768)
         ub_s = kt([P, N], U8, "ub_s")
-        wgt = rt([P, S], F32, "wgt", 43200)
-        h_in = [[kt([P, PACK * SP], BF16, "h_a0"), rt([P, PACK * SP], BF16, "h_a1", 22592),
-                 rt([P, PACK * 2 * SP], BF16, "h_a2", -3968)],
-                [rt([P, PACK * SP], BF16, "h_b0", 47296), rt([P, PACK * SP], BF16, "h_b1", 47360),
-                 kt([P, PACK * 2 * SP], BF16, "h_b2")]]
+        wgt = rt([P, S], F32, "wgt", 34816)
+        h_a = [kt([P, PACK * 2 * SP], BF16, "h_a0"), rt([P, PACK * 2 * SP], BF16, "h_a1", 0)]
+        h_b = [rt([P, PACK * SP], BF16, "h_b0", 4032), rt([P, PACK * SP], BF16, "h_b1", 6016),
+               kt([P, PACK * 2 * SP], BF16, "h_b2")]
         h_w = [kt([P, S], U32, "h_w0"), kt([P, S], U32, "h_w1")]
-        h_s = [kt([P, S], U8, "h_s%d" % b) for b in range(2)]
-        page = [kt([P, T2], F32, "page0"), kt([P, T2], F32, "page1")]
-        y_whole = [kt([P, S], F32, "y%d" % nt) for nt in (0, 2, 3)]
-        y_one = [rt([P, SP], F32, "y1_0", 47424), rt([P, SP], F32, "y1_1", -1920), kt([P, 2 * SP], F32, "y1_2")]
+        h_s = [rt([P, S], U8, "h_s0", 24576), kt([P, S], U8, "h_s1")]
+        page = [kt([P, T2], F32, "page0"), kt([P, T2], F32, "page1"), rt([P, T2], F32, "page2", 41152)]
+        y_whole = [kt([P, S], F32, "y%d" % nt) for nt in range(4)]
+        ya_whole = [kt([P, S], F32, "ya%d" % nt) for nt in range(4)]
+        y_late = rt([P, 2 * SP], F32, "y_late", 39040)
 
         def y(nt, j0, j1):
-            if nt == 1:
-                return y_one[j0 // SP][:]
-            return y_whole[max(nt - 1, 0)][:, j0:j1]
+            if nt == 1 and j0 == 2 * SP:
+                return y_late[:]
+            return y_whole[nt][:, j0:j1]
 
         nc.gpsimd.memset(ub_s[:].bitcast(I32), 0)
         nc.gpsimd.memset(was_raw[:].rearrange("p a c -> p (a c)").bitcast(I32), 0)
@@ -99,15 +99,21 @@ def tile_list_twin_critic_replay_kernel(tc, tab_words, tab_scales, offs, wa4_wor
         scale_rows = tab_scales.rearrange("a (h q r) t -> q (a h) r t", h=2, q=2)
         for q in range(2):
             nc.sync.dma_start(tabs[32 * q + 16:32 * q + 32, :].bitcast(I32), scale_rows[q].bitcast(I32))
-        for q in range(4):
+
+        def load_ub_scales(q):
             nc.sync.dma_start(ub_s[32 * q:32 * q + 4, :].bitcast(I32), ub8_scales[0, 4 * q:4 * q + 4, :].bitcast(I32))
+
+        load_ub_scales(0)
+        load_ub_scales(1)
         load_words(0)
         for q in range(4):
             nc.sync.dma_start(was_raw[32 * q:32 * q + 4, :, :].bitcast(I32),
                               wa4_scales[:, 4 * q:4 * q + 4, :].rearrange("a r c -> r a c").bitcast(I32))
         nc.sync.dma_start(wa_raw[:].bitcast(I32), wa4_words.rearrange("a p c -> p a c").bitcast(I32))
-        load_words(1)
         nc.sync.dma_start(idx2[:], offs2)
+        load_words(1)
+        load_ub_scales(2)
+        load_ub_scales(3)
 
         def gather_words(a, j0, j1):
             nc.vector.tensor_copy(vw[a][:, j0:j1], tabw[a][:].bitcast(U32).indirect(idx[:, j0 // 16:j1 // 16]))
@@ -158,8 +164,11 @@ def tile_list_twin_critic_replay_kernel(tc, tab_words, tab_scales, offs, wa4_wor
                                 start=(a == 0 and t == 0), stop=(a == 1 and t == PACK - 1))
 
         def h_bf(b, j0, j1):
+            if b == 0:
+                s = j0 // (2 * SP)
+                return h_a[s][:, PACK * (j0 - s * 2 * SP):PACK * (j1 - s * 2 * SP)]
             s = min(j0 // SP, 2)
-            return h_in[b][s][:, PACK * (j0 - s * SP):PACK * (j1 - s * SP)]
+            return h_b[s][:, PACK * (j0 - s * SP):PACK * (j1 - s * SP)]
 
         def relu(b, jb, bank, on_vector=False):
             dst = h_bf(b, jb * JB, (jb + 1) * JB).rearrange("p (n t) -> p n t", t=PACK)
@@ -190,9 +199,9 @@ def tile_list_twin_critic_replay_kernel(tc, tab_words, tab_scales, offs, wa4_wor
 
         def value_a(nt, j0, j1, k):
             ya = value(0, nt, j0, j1, k)
-            ya_sb = ring.tile([P, 512], F32, name="ya_sb")
-            nc.scalar.copy(ya_sb[:, 0:j1 - j0], ya)
-            return ya_sb[:, 0:j1 - j0]
+            ya_sb = ya_whole[nt][:, j0:j1]
+            nc.scalar.copy(ya_sb, ya)
+            return ya_sb
 
         def minimum(nt, j0, j1, ya_sb, k):
             nc.vector.tensor_tensor(y(nt, j0, j1), value(1, nt, j0, j1, k), ya_sb, ALU.min)
@@ -201,11 +210,11 @@ def tile_list_twin_critic_replay_kernel(tc, tab_words, tab_scales, offs, wa4_wor
             minimum(nt, j0, j1, value_a(nt, j0, j1, k), k + 1)
 
         def scatter(nt, j0, j1):
-            nc.vector.tensor_tensor(page[nt % 2][:].indirect(idx2[:, j0 // 16:j1 // 16]), y(nt, j0, j1),
+            nc.vector.tensor_tensor(page[nt % 3][:].indirect(idx2[:, j0 // 16:j1 // 16]), y(nt, j0, j1),
                                     wgt[:, j0:j1], ALU.mult)
 
         def store(nt):
-            nc.sync.dma_start(out[nt * P:(nt + 1) * P, :], page[nt % 2][:])
+            nc.sync.dma_start(out[nt * P:(nt + 1) * P, :], page[nt % 3][:])
 
         nc.vector.tensor_copy(vs_top[:], tabs[:].indirect(idx[:]))
         for a in range(2):
@@ -216,83 +225,82 @@ def tile_list_twin_critic_replay_kernel(tc, tab_words, tab_scales, offs, wa4_wor
         load_wb(1, 0, H)
         gather_words(0, 0, S)
         load_ua(0)
+        reorder(wa_w[:], wa_raw[:], 4)
         nc.sync.dma_start(ub_w[:], ub8_words[0].rearrange("p c i -> p (c i)").bitcast(I32))
         nc.sync.dma_start(wgt[:], wgo)
-        reorder(wa_w[:], wa_raw[:], 4)
         reorder(wa_s[:], was_raw[:], 2)
+        nc.gpsimd.memset(page[2][:], 0.0)
         gather_words(1, 0, SP)
         gather_words(1, SP, S)
         hidden(0, 0, 2)
         hidden(0, 1, 3)
-        banks_a = [bank_tile(2 + jb) for jb in range(2)]
+        cast_wb(0, 0, CUT0)
+        cast_wb(0, CUT0, H, True)
+        quant_wb(0, 0, H)
+        hidden(0, 2, 2)
+        hidden(0, 3, 3)
+        banks_a = [bank_tile(2), bank_tile(3)]
         for jb in range(2):
             for a in range(2):
                 for t in range(PACK):
-                    one_pass(0, 2 + jb, banks_a[jb], a, t)
-        cast_wb(0, 0, CUT)
-        cast_wb(0, CUT, H, True)
-        load_ua(1)
-        quant_wb(0, 0, H)
+                    one_pass(0, 4 + jb, banks_a[jb], a, t)
         banks = [bank_tile(k) for k in (0, 1, 6, 7)]
         for jb in range(4):
             for t in range(PACK):
                 one_pass(1, jb, banks[jb], 0, t)
-        cast_wb(1, 0, CUT)
-        cast_wb(1, CUT, H, True)
-        quant_wb(1, 0, H // 2)
-        quant_wb(1, H // 2, H)
-        for t in range(PACK):
-            for jb in range(2):
+        cast_wb(1, 0, CUT1)
+        cast_wb(1, CUT1, H, True)
+        quant_wb(1, 0, H)
+        for jb in range(2):
+            for t in range(PACK):
                 one_pass(1, jb, banks[jb], 1, t)
-        cast_ua(0, 0, P, True)
-        quant_ua(0, 1)
+        cast_ua(0, 0, 2 * P)
+        load_ua(1)
         quant_h(0, 0, SP)
-        ya0 = value_a(0, 0, SP, 4)
-        relu(1, 0, banks[0])
-        relu(1, 1, banks[1], True)
-        quant_h(1, 0, SP)
-        minimum(0, 0, SP, ya0, 5)
-        cast_ua(0, P, 2 * P)
-        quant_ua(1, 2)
-        relu(0, 2, banks_a[0])
-        relu(0, 3, banks_a[1])
+        quant_ua(0, 2)
+        relu(1, 0, banks[0], True)
+        relu(1, 1, banks[1])
         quant_h(0, SP, 2 * SP)
-        ya1 = value_a(1, 0, SP, 2)
+        quant_h(1, 0, SP)
+        ya00 = value_a(0, 0, SP, 0)
+        minimum(0, 0, SP, ya00, 1)
         scatter(0, 0, SP)
         for jb in range(2, 4):
             for t in range(PACK):
                 one_pass(1, jb, banks[jb], 1, t)
             relu(1, jb, banks[jb])
         quant_h(1, SP, 2 * SP)
-        minimum(1, 0, SP, ya1, 3)
+        ya01 = value_a(0, SP, 2 * SP, 4)
+        ya10 = value_a(1, 0, SP, 7)
+        minimum(1, 0, SP, ya10, 0)
+        minimum(0, SP, 2 * SP, ya01, 5)
         scatter(1, 0, SP)
-        values(0, SP, 2 * SP, 4)
-        ya1 = value_a(1, SP, 2 * SP, 2)
         scatter(0, SP, 2 * SP)
-        hidden(1, 4, 0)
-        hidden(1, 5, 1)
-        hidden(1, 6, 6)
-        hidden(1, 7, 7)
-        quant_h(1, 2 * SP, S)
-        hidden(0, 4, 0)
-        hidden(0, 5, 1)
-        hidden(0, 6, 6)
-        hidden(0, 7, 7)
+        relu(0, 4, banks_a[0])
+        relu(0, 5, banks_a[1])
+        hidden(0, 6, 1)
+        hidden(0, 7, 6)
         quant_h(0, 2 * SP, S)
-        minimum(1, SP, 2 * SP, ya1, 3)
-        scatter(1, SP, 2 * SP)
+        for jb, k in zip(range(4, 8), (7, 2, 3, 1)):
+            hidden(1, jb, k)
+        quant_h(1, 2 * SP, S)
+        ya11 = value_a(1, SP, 2 * SP, 1)
+        ya02 = value_a(0, 2 * SP, S, 3)
+        minimum(1, SP, 2 * SP, ya11, 4)
+        minimum(0, 2 * SP, S, ya02, 2)
+        ya12 = value_a(1, 2 * SP, S, 1)
         cast_ua(1, 0, 2 * P)
+        scatter(1, SP, 2 * SP)
         quant_ua(2, 4)
-        values(0, 2 * SP, S, 4)
-        values(1, 2 * SP, S, 2)
+        minimum(1, 2 * SP, S, ya12, 7)
         scatter(0, 2 * SP, S)
         store(0)
-        values(2, 0, 512, 6)
-        values(2, 512, S, 0)
+        minimum(2, 0, 512, value_a(2, 0, 512, 2), 4)
         scatter(1, 2 * SP, S)
         store(1)
-        values(3, 0, 512, 4)
-        values(3, 512, S, 2)
+        minimum(2, 512, S, value_a(2, 512, S, 7), 3)
+        minimum(3, 0, 512, value_a(3, 0, 512, 2), 6)
+        minimum(3, 512, S, value_a(3, 512, S, 7), 5)
         scatter(2, 0, S)
         store(2)
         scatter(3, 0, S)

@@ -52,10 +52,10 @@ def tile_list_twin_critic_replay_kernel(tc, tab_words, tab_scales, offs, wa4_wor
         wa_s = rt([P, 2, H], U8, "wa_s", 14400)
         wb_raw = [rt([P, PACK, H], F32, "wb_raw0", 16320), rt([P, PACK, H], F32, "wb_raw1", 24512)]
         wb_bf = [kt([P, PACK * H], BF16, "wb_bf%d" % a) for a in range(2)]
-        wb_w = [kt([P, H], U32, "wb_w%d" % a) for a in range(2)]
+        wb_w = [kt([P, H], U32, "wb_w0"), rt([P, H], U32, "wb_w1", 49408)]
         wb_s = [kt([P, H], U8, "wb_s%d" % a) for a in range(2)]
         ua_raw = [rt([P, PACK, 2 * P], F32, "ua_raw0", 4096), rt([P, PACK, 2 * P], F32, "ua_raw1", 8128)]
-        ua_bf = [kt([P, 2 * KP], BF16, "ua_bf0"), rt([P, 2 * KP], BF16, "ua_bf1", 38976)]
+        ua_bf = [kt([P, 2 * KP], BF16, "ua_bf0"), rt([P, 2 * KP], BF16, "ua_bf1", 49472)]
         ua_w = kt([P, N], U32, "ua_w")
         ua_s = kt([P, N], U8, "ua_s")
         ub_w = rt([P, N], I32, "ub_w", 32768)
@@ -69,7 +69,7 @@ def tile_list_twin_critic_replay_kernel(tc, tab_words, tab_scales, offs, wa4_wor
         page = [kt([P, T2], F32, "page0"), kt([P, T2], F32, "page1"), rt([P, T2], F32, "page2", 41152)]
         y_whole = [kt([P, S], F32, "y%d" % nt) for nt in range(4)]
         ya_whole = [kt([P, S], F32, "ya%d" % nt) for nt in range(4)]
-        y_late = rt([P, 2 * SP], F32, "y_late", 39040)
+        y_late = rt([P, 2 * SP], F32, "y_late", 49536)
 
         def y(nt, j0, j1):
             if nt == 1 and j0 == 2 * SP:
@@ -104,13 +104,12 @@ def tile_list_twin_critic_replay_kernel(tc, tab_words, tab_scales, offs, wa4_wor
             nc.sync.dma_start(ub_s[32 * q:32 * q + 4, :].bitcast(I32), ub8_scales[0, 4 * q:4 * q + 4, :].bitcast(I32))
 
         load_ub_scales(0)
-        load_ub_scales(1)
         load_words(0)
         for q in range(4):
             nc.sync.dma_start(was_raw[32 * q:32 * q + 4, :, :].bitcast(I32),
                               wa4_scales[:, 4 * q:4 * q + 4, :].rearrange("a r c -> r a c").bitcast(I32))
         nc.sync.dma_start(wa_raw[:].bitcast(I32), wa4_words.rearrange("a p c -> p a c").bitcast(I32))
-        nc.sync.dma_start(idx2[:], offs2)
+        load_ub_scales(1)
         load_words(1)
         load_ub_scales(2)
         load_ub_scales(3)
@@ -150,7 +149,7 @@ def tile_list_twin_critic_replay_kernel(tc, tab_words, tab_scales, offs, wa4_wor
             nc.vector.quantize_mx(out=ua_w[:, cols].bitcast(FP8X4), scales=ua_s[:, cols],
                                   in_=ua_bf[n0 // 2][:, n0 % 2 * KP:(n0 % 2 + n1 - n0) * KP])
 
-        def one_pass(b, jb, bank, a, t):
+        def one_pass(b, jb, bank, a, t, first=0):
             cols = slice(t * P, (t + 1) * P)
             js = slice(jb * JB, (jb + 1) * JB)
             if b == 0:
@@ -161,7 +160,7 @@ def tile_list_twin_critic_replay_kernel(tc, tab_words, tab_scales, offs, wa4_wor
                 lhs_s = wb_s[a][:, cols]
             nc.tensor.matmul_mx(out=bank[:, cols], lhsT=lhs, lhsT_scale=lhs_s, rhs=vw[a][:, js].bitcast(FP8X4),
                                 rhs_scale=vs[:, a, js],
-                                start=(a == 0 and t == 0), stop=(a == 1 and t == PACK - 1))
+                                start=(a == first and t == 0), stop=(a == 1 - first and t == PACK - 1))
 
         def h_bf(b, j0, j1):
             if b == 0:
@@ -178,11 +177,11 @@ def tile_list_twin_critic_replay_kernel(tc, tab_words, tab_scales, offs, wa4_wor
             else:
                 nc.scalar.activation(dst, src, ACT.Relu)
 
-        def hidden(b, jb, k):
+        def hidden(b, jb, k, first=0):
             bank = bank_tile(k)
-            for a in range(2):
+            for a in (first, 1 - first):
                 for t in range(PACK):
-                    one_pass(b, jb, bank, a, t)
+                    one_pass(b, jb, bank, a, t, first)
             relu(b, jb, bank)
 
         def quant_h(b, j0, j1):
@@ -228,14 +227,15 @@ def tile_list_twin_critic_replay_kernel(tc, tab_words, tab_scales, offs, wa4_wor
         reorder(wa_w[:], wa_raw[:], 4)
         nc.sync.dma_start(ub_w[:], ub8_words[0].rearrange("p c i -> p (c i)").bitcast(I32))
         nc.sync.dma_start(wgt[:], wgo)
+        nc.sync.dma_start(idx2[:], offs2)
         reorder(wa_s[:], was_raw[:], 2)
         nc.gpsimd.memset(page[2][:], 0.0)
         gather_words(1, 0, SP)
-        gather_words(1, SP, S)
+        gather_words(1, SP, 2 * SP)
+        gather_words(1, 2 * SP, S)
         hidden(0, 0, 2)
-        hidden(0, 1, 3)
-        cast_wb(0, 0, CUT0)
-        cast_wb(0, CUT0, H, True)
+        hidden(0, 1, 3, 1)
+        cast_wb(0, 0, H, True)
         quant_wb(0, 0, H)
         hidden(0, 2, 2)
         hidden(0, 3, 3)
@@ -284,22 +284,22 @@ def tile_list_twin_critic_replay_kernel(tc, tab_words, tab_scales, offs, wa4_wor
         for jb, k in zip(range(4, 8), (7, 2, 3, 1)):
             hidden(1, jb, k)
         quant_h(1, 2 * SP, S)
-        ya11 = value_a(1, SP, 2 * SP, 1)
+        ya11 = value_a(1, SP, 2 * SP, 2)
         ya02 = value_a(0, 2 * SP, S, 3)
         minimum(1, SP, 2 * SP, ya11, 4)
-        minimum(0, 2 * SP, S, ya02, 2)
-        ya12 = value_a(1, 2 * SP, S, 1)
+        minimum(0, 2 * SP, S, ya02, 1)
+        ya12 = value_a(1, 2 * SP, S, 2)
         cast_ua(1, 0, 2 * P)
         scatter(1, SP, 2 * SP)
         quant_ua(2, 4)
         minimum(1, 2 * SP, S, ya12, 7)
         scatter(0, 2 * SP, S)
         store(0)
-        minimum(2, 0, 512, value_a(2, 0, 512, 2), 4)
+        minimum(2, 0, 512, value_a(2, 0, 512, 1), 4)
         scatter(1, 2 * SP, S)
         store(1)
         minimum(2, 512, S, value_a(2, 512, S, 7), 3)
-        minimum(3, 0, 512, value_a(3, 0, 512, 2), 6)
+        minimum(3, 0, 512, value_a(3, 0, 512, 1), 6)
         minimum(3, 512, S, value_a(3, 512, S, 7), 5)
         scatter(2, 0, S)
         store(2)

@@ -22,7 +22,7 @@ KP = P * PACK
 JB = 128
 SP = 256
 CUT0 = 128
-CUT1 = 160
+CUT1 = 192
 
 
 def tile_list_twin_critic_replay_kernel(tc, tab_words, tab_scales, offs, wa4_words, wa4_scales, wb, ua,
@@ -149,7 +149,7 @@ def tile_list_twin_critic_replay_kernel(tc, tab_words, tab_scales, offs, wa4_wor
             nc.vector.quantize_mx(out=ua_w[:, cols].bitcast(FP8X4), scales=ua_s[:, cols],
                                   in_=ua_bf[n0 // 2][:, n0 % 2 * KP:(n0 % 2 + n1 - n0) * KP])
 
-        def one_pass(b, jb, bank, a, t, first=0):
+        def one_pass(b, jb, bank, a, t, first=0, last=PACK - 1):
             cols = slice(t * P, (t + 1) * P)
             js = slice(jb * JB, (jb + 1) * JB)
             if b == 0:
@@ -160,7 +160,7 @@ def tile_list_twin_critic_replay_kernel(tc, tab_words, tab_scales, offs, wa4_wor
                 lhs_s = wb_s[a][:, cols]
             nc.tensor.matmul_mx(out=bank[:, cols], lhsT=lhs, lhsT_scale=lhs_s, rhs=vw[a][:, js].bitcast(FP8X4),
                                 rhs_scale=vs[:, a, js],
-                                start=(a == first and t == 0), stop=(a == 1 - first and t == PACK - 1))
+                                start=(a == first and t == 0), stop=(a == 1 - first and t == last))
 
         def h_bf(b, j0, j1):
             if b == 0:
@@ -250,10 +250,11 @@ def tile_list_twin_critic_replay_kernel(tc, tab_words, tab_scales, offs, wa4_wor
                 one_pass(1, jb, banks[jb], 0, t)
         cast_wb(1, 0, CUT1)
         cast_wb(1, CUT1, H, True)
-        quant_wb(1, 0, H)
-        for jb in range(2):
-            for t in range(PACK):
-                one_pass(1, jb, banks[jb], 1, t)
+        for half in range(2):
+            quant_wb(1, half * H // 2, (half + 1) * H // 2)
+            for jb in range(2):
+                for t in range(2 * half, 2 * half + 2):
+                    one_pass(1, jb, banks[jb], 1, t)
         cast_ua(0, 0, 2 * P)
         load_ua(1)
         quant_h(0, 0, SP)
@@ -266,8 +267,8 @@ def tile_list_twin_critic_replay_kernel(tc, tab_words, tab_scales, offs, wa4_wor
         minimum(0, 0, SP, ya00, 1)
         scatter(0, 0, SP)
         for jb in range(2, 4):
-            for t in range(PACK):
-                one_pass(1, jb, banks[jb], 1, t)
+            for t in (2, 3, 0, 1):
+                one_pass(1, jb, banks[jb], 1, t, last=1)
             relu(1, jb, banks[jb])
         quant_h(1, SP, 2 * SP)
         ya01 = value_a(0, SP, 2 * SP, 4)

@@ -41,12 +41,12 @@ def tile_list_twin_critic_replay_kernel(tc, tab_words, tab_scales, offs, wa4_wor
 
         idx = keep.tile([P, S // 16], U16, name="idx")
         idx2 = keep.tile([P, S // 16], U16, name="idx2")
-        tabw = [rt([P, T], I32, "tabw0", 8064), kt([P, T], I32, "tabw1")]
+        tabw = [rt([P, T], I32, "tabw0", 8064), rt([P, T], I32, "tabw1", 57472)]
         tabs = rt([P, T], U8, "tabs", 24448)
         vw = [kt([P, S], U32, "vw%d" % a) for a in range(2)]
         vs_top = kt([P, S], U8, "vs_top")
         vs = kt([P, 2, S], U8, "vs")
-        wa_raw = rt([P, 2, 2 * H], U8, "wa_raw", 34752)
+        wa_raw = kt([P, 2, 2 * H], U8, "wa_raw")
         wa_w = rt([P, 2, 2 * H], U8, "wa_w", 12288)
         was_raw = rt([P, 2, H], U8, "was_raw", 41088)
         wa_s = rt([P, 2, H], U8, "wa_s", 14400)
@@ -54,18 +54,28 @@ def tile_list_twin_critic_replay_kernel(tc, tab_words, tab_scales, offs, wa4_wor
         wb_bf = [kt([P, PACK * H], BF16, "wb_bf%d" % a) for a in range(2)]
         wb_w = [kt([P, H], U32, "wb_w0"), rt([P, H], U32, "wb_w1", 49408)]
         wb_s = [kt([P, H], U8, "wb_s%d" % a) for a in range(2)]
-        ua_raw = [rt([P, PACK, 2 * P], F32, "ua_raw0", 4096), rt([P, PACK, 2 * P], F32, "ua_raw1", 8128)]
-        ua_bf = [kt([P, 2 * KP], BF16, "ua_bf0"), rt([P, 2 * KP], BF16, "ua_bf1", 49472)]
+        ua_raw = [rt([P, PACK, 2 * P], F32, "ua_raw0", 4096), rt([P, PACK, 2 * P], F32, "ua_raw1", 53312)]
+        ua_bf = [rt([P, 2 * KP], BF16, "ua_bf0", 53248), rt([P, 2 * KP], BF16, "ua_bf1", 49472)]
         ua_w = kt([P, N], U32, "ua_w")
         ua_s = kt([P, N], U8, "ua_s")
-        ub_w = rt([P, N], I32, "ub_w", 32768)
+        ub_w = rt([P, N], I32, "ub_w", 57536)
         ub_s = kt([P, N], U8, "ub_s")
-        wgt = rt([P, S], F32, "wgt", 34816)
-        h_a = [kt([P, PACK * 2 * SP], BF16, "h_a0"), rt([P, PACK * 2 * SP], BF16, "h_a1", 0)]
-        h_b = [rt([P, PACK * SP], BF16, "h_b0", 4032), rt([P, PACK * SP], BF16, "h_b1", 6016),
+        wgt = rt([P, S], F32, "wgt", 59648)
+        h_a = [kt([P, PACK * 2 * SP], BF16, "h_a0"), rt([P, PACK * 2 * SP], BF16, "h_a1", 4224)]
+        h_b = [rt([P, PACK * SP], BF16, "h_b0", 2112), rt([P, PACK * SP], BF16, "h_b1", 128),
                kt([P, PACK * 2 * SP], BF16, "h_b2")]
-        h_w = [kt([P, S], U32, "h_w0"), kt([P, S], U32, "h_w1")]
-        h_s = [rt([P, S], U8, "h_s0", 24576), kt([P, S], U8, "h_s1")]
+        ha_w = [kt([P, SP], U32, "ha_w0"), kt([P, S - SP], U32, "ha_w1")]
+        ha_s = [rt([P, SP], U8, "ha_s0", 24576), rt([P, S - SP], U8, "ha_s1", 2240)]
+        hb_w = kt([P, S], U32, "hb_w")
+        hb_s = kt([P, S], U8, "hb_s")
+
+        def h_mx(b, j0, j1):
+            if b == 1:
+                return hb_w[:, j0:j1].bitcast(FP8X4), hb_s[:, j0:j1]
+            part = min(j0 // SP, 1)
+            cols = slice(j0 - part * SP, j1 - part * SP)
+            return ha_w[part][:, cols].bitcast(FP8X4), ha_s[part][:, cols]
+
         page = [kt([P, T2], F32, "page0"), kt([P, T2], F32, "page1"), rt([P, T2], F32, "page2", 41152)]
         y_whole = [kt([P, S], F32, "y%d" % nt) for nt in range(4)]
         ya_whole = [kt([P, S], F32, "ya%d" % nt) for nt in range(4)]
@@ -185,15 +195,18 @@ def tile_list_twin_critic_replay_kernel(tc, tab_words, tab_scales, offs, wa4_wor
             relu(b, jb, bank)
 
         def quant_h(b, j0, j1):
-            nc.vector.quantize_mx(out=h_w[b][:, j0:j1].bitcast(FP8X4), scales=h_s[b][:, j0:j1],
-                                  in_=h_bf(b, j0, j1))
+            codes, scales = h_mx(b, j0, j1)
+            nc.vector.quantize_mx(out=codes, scales=scales, in_=h_bf(b, j0, j1))
 
         def value(b, nt, j0, j1, k):
             cols = slice(nt * P, (nt + 1) * P)
             bank = bank_tile(k)
             u_w, u_s = ((ua_w, ua_s), (ub_w, ub_s))[b]
-            nc.tensor.matmul_mx(out=bank[:, 0:j1 - j0], lhsT=u_w[:, cols].bitcast(FP8X4), lhsT_scale=u_s[:, cols],
-                                rhs=h_w[b][:, j0:j1].bitcast(FP8X4), rhs_scale=h_s[b][:, j0:j1], start=True, stop=True)
+            cuts = (j0, SP, j1) if b == 0 and j0 < SP < j1 else (j0, j1)
+            for c0, c1 in zip(cuts, cuts[1:]):
+                codes, scales = h_mx(b, c0, c1)
+                nc.tensor.matmul_mx(out=bank[:, c0 - j0:c1 - j0], lhsT=u_w[:, cols].bitcast(FP8X4),
+                                    lhsT_scale=u_s[:, cols], rhs=codes, rhs_scale=scales, start=True, stop=True)
             return bank[:, 0:j1 - j0]
 
         def value_a(nt, j0, j1, k):
@@ -225,14 +238,17 @@ def tile_list_twin_critic_replay_kernel(tc, tab_words, tab_scales, offs, wa4_wor
         gather_words(0, 0, S)
         load_ua(0)
         reorder(wa_w[:], wa_raw[:], 4)
-        nc.sync.dma_start(ub_w[:], ub8_words[0].rearrange("p c i -> p (c i)").bitcast(I32))
-        nc.sync.dma_start(wgt[:], wgo)
-        nc.sync.dma_start(idx2[:], offs2)
         reorder(wa_s[:], was_raw[:], 2)
         nc.gpsimd.memset(page[2][:], 0.0)
         gather_words(1, 0, SP)
         gather_words(1, SP, 2 * SP)
         gather_words(1, 2 * SP, S)
+        ub_words = ub8_words[0].rearrange("p c i -> p (c i)").bitcast(I32)
+        nc.sync.dma_start(ub_w[:, 0:2 * P], ub_words[:, 0:2 * P])
+        nc.sync.dma_start(wgt[:, 0:SP], wgo[:, 0:SP])
+        nc.sync.dma_start(idx2[:], offs2)
+        nc.sync.dma_start(wgt[:, SP:S], wgo[:, SP:S])
+        nc.sync.dma_start(ub_w[:, 2 * P:N], ub_words[:, 2 * P:N])
         hidden(0, 0, 2)
         hidden(0, 1, 3, 1)
         cast_wb(0, 0, H, True)
@@ -255,14 +271,16 @@ def tile_list_twin_critic_replay_kernel(tc, tab_words, tab_scales, offs, wa4_wor
             for jb in range(2):
                 for t in range(2 * half, 2 * half + 2):
                     one_pass(1, jb, banks[jb], 1, t)
-        cast_ua(0, 0, 2 * P)
-        load_ua(1)
+        cast_ua(0, P, 2 * P)
+        cast_ua(0, 0, P, True)
         quant_h(0, 0, SP)
-        quant_ua(0, 2)
+        quant_ua(0, 1)
         relu(1, 0, banks[0], True)
         relu(1, 1, banks[1])
-        quant_h(0, SP, 2 * SP)
+        quant_ua(1, 2)
+        load_ua(1)
         quant_h(1, 0, SP)
+        quant_h(0, SP, 2 * SP)
         ya00 = value_a(0, 0, SP, 0)
         minimum(0, 0, SP, ya00, 1)
         scatter(0, 0, SP)
@@ -273,35 +291,35 @@ def tile_list_twin_critic_replay_kernel(tc, tab_words, tab_scales, offs, wa4_wor
         quant_h(1, SP, 2 * SP)
         ya01 = value_a(0, SP, 2 * SP, 4)
         ya10 = value_a(1, 0, SP, 7)
-        minimum(1, 0, SP, ya10, 0)
-        minimum(0, SP, 2 * SP, ya01, 5)
-        scatter(1, 0, SP)
-        scatter(0, SP, 2 * SP)
         relu(0, 4, banks_a[0])
         relu(0, 5, banks_a[1])
+        minimum(1, 0, SP, ya10, 2)
+        minimum(0, SP, 2 * SP, ya01, 3)
+        scatter(1, 0, SP)
+        scatter(0, SP, 2 * SP)
         hidden(0, 6, 1)
         hidden(0, 7, 6)
         quant_h(0, 2 * SP, S)
-        for jb, k in zip(range(4, 8), (7, 2, 3, 1)):
+        for jb, k in zip(range(4, 8), (7, 0, 4, 1)):
             hidden(1, jb, k)
         quant_h(1, 2 * SP, S)
-        ya11 = value_a(1, SP, 2 * SP, 2)
-        ya02 = value_a(0, 2 * SP, S, 3)
-        minimum(1, SP, 2 * SP, ya11, 4)
+        ya11 = value_a(1, SP, 2 * SP, 0)
+        ya02 = value_a(0, 2 * SP, S, 4)
+        minimum(1, SP, 2 * SP, ya11, 5)
         minimum(0, 2 * SP, S, ya02, 1)
-        ya12 = value_a(1, 2 * SP, S, 2)
+        ya12 = value_a(1, 2 * SP, S, 0)
         cast_ua(1, 0, 2 * P)
         scatter(1, SP, 2 * SP)
         quant_ua(2, 4)
         minimum(1, 2 * SP, S, ya12, 7)
         scatter(0, 2 * SP, S)
         store(0)
-        minimum(2, 0, 512, value_a(2, 0, 512, 1), 4)
+        minimum(2, 0, 512, value_a(2, 0, 512, 2), 5)
         scatter(1, 2 * SP, S)
         store(1)
-        minimum(2, 512, S, value_a(2, 512, S, 7), 3)
-        minimum(3, 0, 512, value_a(3, 0, 512, 1), 6)
-        minimum(3, 512, S, value_a(3, 512, S, 7), 5)
+        minimum(2, 512, S, value_a(2, 512, S, 4), 1)
+        minimum(3, 0, 512, value_a(3, 0, 512, 0), 6)
+        minimum(3, 512, S, value_a(3, 512, S, 2), 3)
         scatter(2, 0, S)
         store(2)
         scatter(3, 0, S)

@@ -41,53 +41,65 @@ def tile_list_twin_critic_replay_kernel(tc, tab_words, tab_scales, offs, wa4_wor
 
         idx = keep.tile([P, S // 16], U16, name="idx")
         idx2 = keep.tile([P, S // 16], U16, name="idx2")
-        tabw = [rt([P, T], I32, "tabw0", 8064), rt([P, T], I32, "tabw1", 57472)]
-        tabs = rt([P, T], U8, "tabs", 24448)
+        tabw = [rt([P, T], I32, "tabw0", 8192), rt([P, T], I32, "tabw1", 44032)]
+        tabs = rt([P, T], U8, "tabs", 24576)
         vw = [kt([P, S], U32, "vw%d" % a) for a in range(2)]
         vs_top = kt([P, S], U8, "vs_top")
-        vs = kt([P, 2, S], U8, "vs")
+        vs = [kt([P, 2, S // 2], U8, "vs0"), rt([P, 2, S // 2], U8, "vs1", 50368)]
         wa_raw = kt([P, 2, 2 * H], U8, "wa_raw")
         wa_w = rt([P, 2, 2 * H], U8, "wa_w", 12288)
-        was_raw = rt([P, 2, H], U8, "was_raw", 41088)
+        was_raw = rt([P, 2, H], U8, "was_raw", 34816)
         wa_s = rt([P, 2, H], U8, "wa_s", 14400)
-        wb_raw = [rt([P, PACK, H], F32, "wb_raw0", 16320), rt([P, PACK, H], F32, "wb_raw1", 24512)]
+        wb_raw = [rt([P, PACK, H], F32, "wb_raw0", 16448), rt([P, PACK, H], F32, "wb_raw1", 26560)]
         wb_bf = [kt([P, PACK * H], BF16, "wb_bf%d" % a) for a in range(2)]
-        wb_w = [kt([P, H], U32, "wb_w0"), rt([P, H], U32, "wb_w1", 49408)]
+        wb_w = [kt([P, H], U32, "wb_w%d" % a) for a in range(2)]
         wb_s = [kt([P, H], U8, "wb_s%d" % a) for a in range(2)]
-        ua_raw = [rt([P, PACK, 2 * P], F32, "ua_raw0", 4096), rt([P, PACK, 2 * P], F32, "ua_raw1", 53312)]
-        ua_bf = [rt([P, 2 * KP], BF16, "ua_bf0", 53248), rt([P, 2 * KP], BF16, "ua_bf1", 49472)]
+        ua_raw = [rt([P, PACK, 2 * P], F32, "ua_raw0", 4160), rt([P, PACK, 2 * P], F32, "ua_raw1", 51456)]
+        ua_bf = [kt([P, 2 * KP], BF16, "ua_bf0"), rt([P, 2 * KP], BF16, "ua_bf1", 68672)]
         ua_w = kt([P, N], U32, "ua_w")
-        ua_s = kt([P, N], U8, "ua_s")
-        ub_w = rt([P, N], I32, "ub_w", 57536)
+        ua_s = [kt([P, 2 * P], U8, "ua_s%d" % h) for h in range(2)]
+        ub_w = rt([P, N], I32, "ub_w", 44096)
         ub_s = kt([P, N], U8, "ub_s")
-        wgt = rt([P, S], F32, "wgt", 59648)
-        h_a = [kt([P, PACK * 2 * SP], BF16, "h_a0"), rt([P, PACK * 2 * SP], BF16, "h_a1", 4224)]
-        h_b = [rt([P, PACK * SP], BF16, "h_b0", 2112), rt([P, PACK * SP], BF16, "h_b1", 128),
-               kt([P, PACK * 2 * SP], BF16, "h_b2")]
-        ha_w = [kt([P, SP], U32, "ha_w0"), kt([P, S - SP], U32, "ha_w1")]
-        ha_s = [rt([P, SP], U8, "ha_s0", 24576), rt([P, S - SP], U8, "ha_s1", 2240)]
+        wgt = rt([P, S], F32, "wgt", 46208)
+        A_CUTS = (0, 2 * SP, 3 * SP, S)
+        B_CUTS = (0, SP, 2 * SP, S)
+        h_a = [kt([P, PACK * 2 * SP], BF16, "h_a0"), rt([P, PACK * SP], BF16, "h_a1", 72640),
+               kt([P, PACK * SP], BF16, "h_a2")]
+        h_b = [rt([P, PACK * SP], BF16, "h_b0", 4736), rt([P, PACK * SP], BF16, "h_b1", 2752),
+               rt([P, PACK * 2 * SP], BF16, "h_b2", 60416)]
+        ha_w = [kt([P, SP], U32, "ha_w0"), rt([P, S - SP], U32, "ha_w1", 6720)]
+        ha_s = kt([P, S], U8, "ha_s")
         hb_w = kt([P, S], U32, "hb_w")
         hb_s = kt([P, S], U8, "hb_s")
+
+        def part_of(b, j0):
+            cuts = (A_CUTS, B_CUTS)[b]
+            part = max(i for i in range(len(cuts) - 1) if cuts[i] <= j0)
+            return part, cuts[part]
 
         def h_mx(b, j0, j1):
             if b == 1:
                 return hb_w[:, j0:j1].bitcast(FP8X4), hb_s[:, j0:j1]
             part = min(j0 // SP, 1)
-            cols = slice(j0 - part * SP, j1 - part * SP)
-            return ha_w[part][:, cols].bitcast(FP8X4), ha_s[part][:, cols]
+            return ha_w[part][:, j0 - part * SP:j1 - part * SP].bitcast(FP8X4), ha_s[:, j0:j1]
 
-        page = [kt([P, T2], F32, "page0"), kt([P, T2], F32, "page1"), rt([P, T2], F32, "page2", 41152)]
-        y_whole = [kt([P, S], F32, "y%d" % nt) for nt in range(4)]
-        ya_whole = [kt([P, S], F32, "ya%d" % nt) for nt in range(4)]
-        y_late = rt([P, 2 * SP], F32, "y_late", 49536)
+        page = [kt([P, T2], F32, "page0"), kt([P, T2], F32, "page1"), rt([P, T2], F32, "page2", 35776)]
+        y_pair = [kt([P, 2 * SP], F32, "y_pair0"), rt([P, 2 * SP], F32, "y_pair1", 74624)]
+        ya_pair = [rt([P, 2 * SP], F32, "ya_pair0", 70656), kt([P, 2 * SP], F32, "ya_pair1")]
+        y_end = [kt([P, 2 * SP], F32, "y_end%d" % nt) for nt in range(2)]
+        y_whole = [rt([P, S], F32, "y2", 56384), rt([P, S], F32, "y3", 64448)]
+        ya_half = {(nt, j0): kt([P, 2 * SP], F32, "ya%d_%d" % (nt, j0))
+                   for nt in range(4) for j0 in (0, 2 * SP) if nt >= 2 or j0}
 
         def y(nt, j0, j1):
-            if nt == 1 and j0 == 2 * SP:
-                return y_late[:]
-            return y_whole[nt][:, j0:j1]
+            if nt >= 2:
+                return y_whole[nt - 2][:, j0:j1]
+            if j0 >= 2 * SP:
+                return y_end[nt][:]
+            return y_pair[j0 // SP][:, nt * SP:(nt + 1) * SP]
 
-        nc.gpsimd.memset(ub_s[:].bitcast(I32), 0)
-        nc.gpsimd.memset(was_raw[:].rearrange("p a c -> p (a c)").bitcast(I32), 0)
+        nc.vector.memset(was_raw[:].rearrange("p a c -> p (a c)").bitcast(I32), 0)
+        nc.vector.memset(ub_s[:].bitcast(I32), 0)
         for p0, p1 in ((0, 16), (32, 48), (64, 128)):
             nc.gpsimd.memset(tabs[p0:p1, :].bitcast(I32), 0)
         for i in range(2):
@@ -113,16 +125,15 @@ def tile_list_twin_critic_replay_kernel(tc, tab_words, tab_scales, offs, wa4_wor
         def load_ub_scales(q):
             nc.sync.dma_start(ub_s[32 * q:32 * q + 4, :].bitcast(I32), ub8_scales[0, 4 * q:4 * q + 4, :].bitcast(I32))
 
-        load_ub_scales(0)
         load_words(0)
         for q in range(4):
             nc.sync.dma_start(was_raw[32 * q:32 * q + 4, :, :].bitcast(I32),
                               wa4_scales[:, 4 * q:4 * q + 4, :].rearrange("a r c -> r a c").bitcast(I32))
         nc.sync.dma_start(wa_raw[:].bitcast(I32), wa4_words.rearrange("a p c -> p a c").bitcast(I32))
-        load_ub_scales(1)
+        load_ub_scales(0)
         load_words(1)
+        load_ub_scales(1)
         load_ub_scales(2)
-        load_ub_scales(3)
 
         def gather_words(a, j0, j1):
             nc.vector.tensor_copy(vw[a][:, j0:j1], tabw[a][:].bitcast(U32).indirect(idx[:, j0 // 16:j1 // 16]))
@@ -156,8 +167,7 @@ def tile_list_twin_critic_replay_kernel(tc, tab_words, tab_scales, offs, wa4_wor
 
         def quant_ua(n0, n1):
             cols = slice(n0 * P, n1 * P)
-            nc.vector.quantize_mx(out=ua_w[:, cols].bitcast(FP8X4), scales=ua_s[:, cols],
-                                  in_=ua_bf[n0 // 2][:, n0 % 2 * KP:(n0 % 2 + n1 - n0) * KP])
+            nc.vector.quantize_mx(out=ua_w[:, cols].bitcast(FP8X4), scales=ua_s[n0 // 2][:], in_=ua_bf[n0 // 2][:])
 
         def one_pass(b, jb, bank, a, t, first=0, last=PACK - 1):
             cols = slice(t * P, (t + 1) * P)
@@ -169,15 +179,12 @@ def tile_list_twin_critic_replay_kernel(tc, tab_words, tab_scales, offs, wa4_wor
                 lhs = wb_w[a][:, cols].bitcast(FP8X4)
                 lhs_s = wb_s[a][:, cols]
             nc.tensor.matmul_mx(out=bank[:, cols], lhsT=lhs, lhsT_scale=lhs_s, rhs=vw[a][:, js].bitcast(FP8X4),
-                                rhs_scale=vs[:, a, js],
+                                rhs_scale=vs[jb // 4][:, a, jb % 4 * JB:(jb % 4 + 1) * JB],
                                 start=(a == first and t == 0), stop=(a == 1 - first and t == last))
 
         def h_bf(b, j0, j1):
-            if b == 0:
-                s = j0 // (2 * SP)
-                return h_a[s][:, PACK * (j0 - s * 2 * SP):PACK * (j1 - s * 2 * SP)]
-            s = min(j0 // SP, 2)
-            return h_b[s][:, PACK * (j0 - s * SP):PACK * (j1 - s * SP)]
+            part, base = part_of(b, j0)
+            return (h_a, h_b)[b][part][:, PACK * (j0 - base):PACK * (j1 - base)]
 
         def relu(b, jb, bank, on_vector=False):
             dst = h_bf(b, jb * JB, (jb + 1) * JB).rearrange("p (n t) -> p n t", t=PACK)
@@ -187,56 +194,83 @@ def tile_list_twin_critic_replay_kernel(tc, tab_words, tab_scales, offs, wa4_wor
             else:
                 nc.scalar.activation(dst, src, ACT.Relu)
 
-        def hidden(b, jb, k, first=0):
+        def block(b, jb, k, first=0):
             bank = bank_tile(k)
             for a in (first, 1 - first):
                 for t in range(PACK):
                     one_pass(b, jb, bank, a, t, first)
-            relu(b, jb, bank)
+            return bank
 
         def quant_h(b, j0, j1):
             codes, scales = h_mx(b, j0, j1)
             nc.vector.quantize_mx(out=codes, scales=scales, in_=h_bf(b, j0, j1))
 
-        def value(b, nt, j0, j1, k):
+        def product(b, nt, j0, j1, dst):
             cols = slice(nt * P, (nt + 1) * P)
+            if b == 0:
+                u_w, u_s = ua_w[:, cols], ua_s[nt // 2][:, nt % 2 * P:(nt % 2 + 1) * P]
+            else:
+                u_w, u_s = ub_w[:, cols], ub_s[:, cols]
+            codes, scales = h_mx(b, j0, j1)
+            nc.tensor.matmul_mx(out=dst, lhsT=u_w.bitcast(FP8X4), lhsT_scale=u_s, rhs=codes, rhs_scale=scales,
+                                start=True, stop=True)
+
+        def value_pair(b, s, k):
             bank = bank_tile(k)
-            u_w, u_s = ((ua_w, ua_s), (ub_w, ub_s))[b]
-            cuts = (j0, SP, j1) if b == 0 and j0 < SP < j1 else (j0, j1)
-            for c0, c1 in zip(cuts, cuts[1:]):
-                codes, scales = h_mx(b, c0, c1)
-                nc.tensor.matmul_mx(out=bank[:, c0 - j0:c1 - j0], lhsT=u_w[:, cols].bitcast(FP8X4),
-                                    lhsT_scale=u_s[:, cols], rhs=codes, rhs_scale=scales, start=True, stop=True)
-            return bank[:, 0:j1 - j0]
+            for nt in range(2):
+                product(b, nt, s * SP, (s + 1) * SP, bank[:, nt * SP:(nt + 1) * SP])
+            return bank
 
-        def value_a(nt, j0, j1, k):
-            ya = value(0, nt, j0, j1, k)
-            ya_sb = ya_whole[nt][:, j0:j1]
-            nc.scalar.copy(ya_sb, ya)
-            return ya_sb
+        def value_half(b, nt, j0, k):
+            bank = bank_tile(k)
+            if b == 0 and j0 == 0:
+                for c in range(2):
+                    product(b, nt, c * SP, (c + 1) * SP, bank[:, c * SP:(c + 1) * SP])
+            else:
+                product(b, nt, j0, j0 + 2 * SP, bank[:])
+            return bank
 
-        def minimum(nt, j0, j1, ya_sb, k):
-            nc.vector.tensor_tensor(y(nt, j0, j1), value(1, nt, j0, j1, k), ya_sb, ALU.min)
+        def keep_a(nt, j0, k):
+            nc.scalar.copy(ya_half[nt, j0][:], value_half(0, nt, j0, k)[:])
 
-        def values(nt, j0, j1, k):
-            minimum(nt, j0, j1, value_a(nt, j0, j1, k), k + 1)
+        def minimum(dst, bank, ya_sb):
+            nc.vector.tensor_tensor(dst, bank, ya_sb, ALU.min)
+
+        def min_pair(s, bank):
+            for nt in range(2):
+                cols = slice(nt * SP, (nt + 1) * SP)
+                minimum(y_pair[s][:, cols], bank[:, cols], ya_pair[s][:, cols])
+
+        def min_half(nt, j0, bank):
+            minimum(y(nt, j0, j0 + 2 * SP), bank[:], ya_half[nt, j0][:])
 
         def scatter(nt, j0, j1):
             nc.vector.tensor_tensor(page[nt % 3][:].indirect(idx2[:, j0 // 16:j1 // 16]), y(nt, j0, j1),
                                     wgt[:, j0:j1], ALU.mult)
 
         def store(nt):
-            nc.sync.dma_start(out[nt * P:(nt + 1) * P, :], page[nt % 3][:])
+            if nt < 3:
+                nc.sync.dma_start(out[nt * P:(nt + 1) * P, :], page[nt % 3][:])
+                return
+            for c, queue in enumerate((nc.sync, nc.scalar)):
+                cols = slice(c * T2 // 2, (c + 1) * T2 // 2)
+                queue.dma_start(out[nt * P:(nt + 1) * P, cols], page[nt % 3][:, cols])
 
         nc.vector.tensor_copy(vs_top[:], tabs[:].indirect(idx[:]))
-        for a in range(2):
-            for h in range(2):
-                p0 = 16 + 8 * a + 4 * h
-                nc.sync.dma_start(vs[64 * h:64 * h + 64, a, :].bitcast(I32), vs_top[p0:p0 + 64, :].bitcast(I32))
+
+        def move_scales(c):
+            for a in range(2):
+                for h in range(2):
+                    p0 = 16 + 8 * a + 4 * h
+                    nc.sync.dma_start(vs[c][64 * h:64 * h + 64, a, :].bitcast(I32),
+                                      vs_top[p0:p0 + 64, c * S // 2:(c + 1) * S // 2].bitcast(I32))
+
+        move_scales(0)
         load_wb(0, 0, H)
         load_wb(1, 0, H)
         gather_words(0, 0, S)
         load_ua(0)
+        load_ub_scales(3)
         reorder(wa_w[:], wa_raw[:], 4)
         reorder(wa_s[:], was_raw[:], 2)
         nc.gpsimd.memset(page[2][:], 0.0)
@@ -247,23 +281,20 @@ def tile_list_twin_critic_replay_kernel(tc, tab_words, tab_scales, offs, wa4_wor
         nc.sync.dma_start(ub_w[:, 0:2 * P], ub_words[:, 0:2 * P])
         nc.sync.dma_start(wgt[:, 0:SP], wgo[:, 0:SP])
         nc.sync.dma_start(idx2[:], offs2)
+        move_scales(1)
+        load_ua(1)
         nc.sync.dma_start(wgt[:, SP:S], wgo[:, SP:S])
         nc.sync.dma_start(ub_w[:, 2 * P:N], ub_words[:, 2 * P:N])
-        hidden(0, 0, 2)
-        hidden(0, 1, 3, 1)
+        for jb in range(4):
+            relu(0, jb, block(0, jb, 2 + jb, min(jb, 1)))
         cast_wb(0, 0, H, True)
+        quant_h(0, 0, SP)
         quant_wb(0, 0, H)
-        hidden(0, 2, 2)
-        hidden(0, 3, 3)
-        banks_a = [bank_tile(2), bank_tile(3)]
-        for jb in range(2):
-            for a in range(2):
-                for t in range(PACK):
-                    one_pass(0, 4 + jb, banks_a[jb], a, t)
         banks = [bank_tile(k) for k in (0, 1, 6, 7)]
         for jb in range(4):
             for t in range(PACK):
                 one_pass(1, jb, banks[jb], 0, t)
+        late_a = {}
         cast_wb(1, 0, CUT1)
         cast_wb(1, CUT1, H, True)
         for half in range(2):
@@ -271,56 +302,55 @@ def tile_list_twin_critic_replay_kernel(tc, tab_words, tab_scales, offs, wa4_wor
             for jb in range(2):
                 for t in range(2 * half, 2 * half + 2):
                     one_pass(1, jb, banks[jb], 1, t)
-        cast_ua(0, P, 2 * P)
-        cast_ua(0, 0, P, True)
-        quant_h(0, 0, SP)
-        quant_ua(0, 1)
+        cast_ua(0, 0, P)
+        cast_ua(0, P, 2 * P, True)
+        quant_ua(0, 2)
         relu(1, 0, banks[0], True)
         relu(1, 1, banks[1])
-        quant_ua(1, 2)
-        load_ua(1)
+        ya0 = value_pair(0, 0, 2)
         quant_h(1, 0, SP)
+        yb0 = value_pair(1, 0, 4)
+        nc.scalar.copy(ya_pair[0][:], ya0[:])
         quant_h(0, SP, 2 * SP)
-        ya00 = value_a(0, 0, SP, 0)
-        minimum(0, 0, SP, ya00, 1)
+        nc.scalar.copy(ya_pair[1][:], value_pair(0, 1, 3)[:])
+        min_pair(0, yb0)
         scatter(0, 0, SP)
+        scatter(1, 0, SP)
         for jb in range(2, 4):
             for t in (2, 3, 0, 1):
                 one_pass(1, jb, banks[jb], 1, t, last=1)
             relu(1, jb, banks[jb])
-        quant_h(1, SP, 2 * SP)
-        ya01 = value_a(0, SP, 2 * SP, 4)
-        ya10 = value_a(1, 0, SP, 7)
-        relu(0, 4, banks_a[0])
-        relu(0, 5, banks_a[1])
-        minimum(1, 0, SP, ya10, 2)
-        minimum(0, SP, 2 * SP, ya01, 3)
-        scatter(1, 0, SP)
-        scatter(0, SP, 2 * SP)
-        hidden(0, 6, 1)
-        hidden(0, 7, 6)
-        quant_h(0, 2 * SP, S)
-        for jb, k in zip(range(4, 8), (7, 0, 4, 1)):
-            hidden(1, jb, k)
-        quant_h(1, 2 * SP, S)
-        ya11 = value_a(1, SP, 2 * SP, 0)
-        ya02 = value_a(0, 2 * SP, S, 4)
-        minimum(1, SP, 2 * SP, ya11, 5)
-        minimum(0, 2 * SP, S, ya02, 1)
-        ya12 = value_a(1, 2 * SP, S, 0)
         cast_ua(1, 0, 2 * P)
-        scatter(1, SP, 2 * SP)
+        for jb, k in ((4, 5), (5, 2), (6, 3), (7, 4)):
+            late_a[jb] = block(0, jb, k)
+        late_b = {4: block(1, 4, 6), 5: block(1, 5, 7)}
+        for jb in range(4, 6):
+            relu(0, jb, late_a[jb])
+        quant_h(1, SP, 2 * SP)
+        yb1 = value_pair(1, 1, 0)
         quant_ua(2, 4)
-        minimum(1, 2 * SP, S, ya12, 7)
-        scatter(0, 2 * SP, S)
-        store(0)
-        minimum(2, 0, 512, value_a(2, 0, 512, 2), 5)
-        scatter(1, 2 * SP, S)
-        store(1)
-        minimum(2, 512, S, value_a(2, 512, S, 4), 1)
-        minimum(3, 0, 512, value_a(3, 0, 512, 0), 6)
-        minimum(3, 512, S, value_a(3, 512, S, 2), 3)
-        scatter(2, 0, S)
-        store(2)
-        scatter(3, 0, S)
-        store(3)
+        quant_h(0, 2 * SP, 3 * SP)
+        min_pair(1, yb1)
+        scatter(0, SP, 2 * SP)
+        scatter(1, SP, 2 * SP)
+        for jb in range(6, 8):
+            relu(0, jb, late_a[jb])
+        late_b[6] = block(1, 6, 5)
+        late_b[7] = block(1, 7, 2)
+        for jb in range(4, 8):
+            relu(1, jb, late_b[jb])
+        keep_a(2, 0, 1)
+        keep_a(3, 0, 3)
+        yb20 = value_half(1, 2, 0, 4)
+        yb30 = value_half(1, 3, 0, 6)
+        quant_h(0, 3 * SP, S)
+        for nt, k in enumerate((0, 7, 5, 2)):
+            keep_a(nt, 2 * SP, k)
+        quant_h(1, 2 * SP, S)
+        min_half(2, 0, yb20)
+        min_half(3, 0, yb30)
+        for nt, k in enumerate((1, 3, 4, 6)):
+            min_half(nt, 2 * SP, value_half(1, nt, 2 * SP, k))
+        for nt in range(4):
+            scatter(nt, 0 if nt >= 2 else 2 * SP, S)
+            store(nt)

from contextlib import ExitStack

import concourse.mybir as mybir

K, H, N, T, S, T2 = 1024, 512, 512, 2048, 1024, 2048
FLOPS = 2 * S * (2 * K * H + 2 * H * N)

F32 = mybir.dt.float32
BF16 = mybir.dt.bfloat16
I32 = mybir.dt.int32
U32 = mybir.dt.uint32
U16 = mybir.dt.uint16
U8 = mybir.dt.uint8
FP8X4 = mybir.dt.float8_e4m3fn_x4
FP4X4 = mybir.dt.float4_e2m1fn_x4
ACT = mybir.ActivationFunctionType
ALU = mybir.AluOpType

P = 128
PACK = 4
KP = P * PACK
JB = 128
SP = 256
CUT0 = 128
CUT1 = 192


def tile_list_twin_critic_replay_kernel(tc, tab_words, tab_scales, offs, wa4_words, wa4_scales, wb, ua,
                                                 ub8_words, ub8_scales, wgo, offs2, out):
    nc = tc.nc
    with ExitStack() as ctx:
        keep = ctx.enter_context(tc.tile_pool(name="keep", bufs=1))
        reuse = ctx.enter_context(tc.tile_pool(name="reuse", bufs=1))
        psum = ctx.enter_context(tc.psum_pool(name="psum", bufs=1))

        def kt(shape, dtype, name):
            return keep.tile(shape, dtype, name=name, align_bytes=64)

        def rt(shape, dtype, name, offset):
            return reuse.tile(shape, dtype, name=name, align_bytes=64, offset=offset)

        idx = keep.tile([P, S // 16], U16, name="idx")
        idx2 = keep.tile([P, S // 16], U16, name="idx2")
        tabw = [rt([P, T], I32, "tabw0", 8192), rt([P, T], I32, "tabw1", 44032)]
        tabs = rt([P, T], U8, "tabs", 24576)
        vw = [kt([P, S], U32, "vw%d" % a) for a in range(2)]
        vs_top = kt([P, S], U8, "vs_top")
        vs = [kt([P, 2, S // 2], U8, "vs0"), rt([P, 2, S // 2], U8, "vs1", 50368)]
        wa_raw = kt([P, 2, 2 * H], U8, "wa_raw")
        wa_w = rt([P, 2, 2 * H], U8, "wa_w", 12288)
        was_raw = rt([P, 2, H], U8, "was_raw", 34816)
        wa_s = rt([P, 2, H], U8, "wa_s", 14400)
        wb_raw = [rt([P, PACK, H], F32, "wb_raw0", 16448), rt([P, PACK, H], F32, "wb_raw1", 26560)]
        wb_bf = [kt([P, PACK * H], BF16, "wb_bf%d" % a) for a in range(2)]
        wb_w = [kt([P, H], U32, "wb_w%d" % a) for a in range(2)]
        wb_s = [kt([P, H], U8, "wb_s%d" % a) for a in range(2)]
        ua_raw = [rt([P, PACK, 2 * P], F32, "ua_raw0", 4160), rt([P, PACK, 2 * P], F32, "ua_raw1", 51456)]
        ua_bf = [kt([P, 2 * KP], BF16, "ua_bf0"), rt([P, 2 * KP], BF16, "ua_bf1", 68672)]
        ua_w = kt([P, N], U32, "ua_w")
        ua_s = [kt([P, 2 * P], U8, "ua_s%d" % h) for h in range(2)]
        ub_w = rt([P, N], I32, "ub_w", 44096)
        ub_s = kt([P, N], U8, "ub_s")
        wgt = rt([P, S], F32, "wgt", 46208)
        A_CUTS = (0, 2 * SP, 3 * SP, S)
        B_CUTS = (0, SP, 2 * SP, S)
        h_a = [kt([P, PACK * 2 * SP], BF16, "h_a0"), rt([P, PACK * SP], BF16, "h_a1", 72640),
               kt([P, PACK * SP], BF16, "h_a2")]
        h_b = [rt([P, PACK * SP], BF16, "h_b0", 4736), rt([P, PACK * SP], BF16, "h_b1", 2752),
               rt([P, PACK * 2 * SP], BF16, "h_b2", 60416)]
        ha_w = [kt([P, SP], U32, "ha_w0"), rt([P, S - SP], U32, "ha_w1", 6720)]
        ha_s = kt([P, S], U8, "ha_s")
        hb_w = kt([P, S], U32, "hb_w")
        hb_s = kt([P, S], U8, "hb_s")

        def part_of(b, j0):
            cuts = (A_CUTS, B_CUTS)[b]
            part = max(i for i in range(len(cuts) - 1) if cuts[i] <= j0)
            return part, cuts[part]

        def h_mx(b, j0, j1):
            if b == 1:
                return hb_w[:, j0:j1].bitcast(FP8X4), hb_s[:, j0:j1]
            part = min(j0 // SP, 1)
            return ha_w[part][:, j0 - part * SP:j1 - part * SP].bitcast(FP8X4), ha_s[:, j0:j1]

        page = [kt([P, T2], F32, "page0"), kt([P, T2], F32, "page1"), rt([P, T2], F32, "page2", 35776)]
        y_pair = [kt([P, 2 * SP], F32, "y_pair0"), rt([P, 2 * SP], F32, "y_pair1", 74624)]
        ya_pair = [rt([P, 2 * SP], F32, "ya_pair0", 70656), kt([P, 2 * SP], F32, "ya_pair1")]
        y_end = [kt([P, 2 * SP], F32, "y_end%d" % nt) for nt in range(2)]
        y_whole = [rt([P, S], F32, "y2", 56384), rt([P, S], F32, "y3", 64448)]
        ya_half = {(nt, j0): kt([P, 2 * SP], F32, "ya%d_%d" % (nt, j0))
                   for nt in range(4) for j0 in (0, 2 * SP) if nt >= 2 or j0}

        def y(nt, j0, j1):
            if nt >= 2:
                return y_whole[nt - 2][:, j0:j1]
            if j0 >= 2 * SP:
                return y_end[nt][:]
            return y_pair[j0 // SP][:, nt * SP:(nt + 1) * SP]

        nc.vector.memset(was_raw[:].rearrange("p a c -> p (a c)").bitcast(I32), 0)
        nc.vector.memset(ub_s[:].bitcast(I32), 0)
        for p0, p1 in ((0, 16), (32, 48), (64, 128)):
            nc.gpsimd.memset(tabs[p0:p1, :].bitcast(I32), 0)
        for i in range(2):
            nc.gpsimd.memset(page[i][:], 0.0)

        def load_words(a):
            nc.sync.dma_start(tabw[a][:], tab_words[a].rearrange("p t i -> p (t i)").bitcast(I32))

        def load_wb(a, c0, c1):
            nc.sync.dma_start(wb_raw[a][:, :, c0:c1],
                              wb[a * KP:(a + 1) * KP, c0:c1].rearrange("(p j) c -> p j c", j=PACK))

        def load_ua(h):
            rows = ua.rearrange("(g t i) n -> t g i n", t=PACK, i=8)
            for t in range(PACK):
                nc.sync.dma_start(ua_raw[h][:, t, :], rows[t][:, :, h * 2 * P:(h + 1) * 2 * P])

        nc.sync.dma_start(idx[:], offs)
        scale_rows = tab_scales.rearrange("a (h q r) t -> q (a h) r t", h=2, q=2)
        for q in range(2):
            nc.sync.dma_start(tabs[32 * q + 16:32 * q + 32, :].bitcast(I32), scale_rows[q].bitcast(I32))

        def load_ub_scales(q):
            nc.sync.dma_start(ub_s[32 * q:32 * q + 4, :].bitcast(I32), ub8_scales[0, 4 * q:4 * q + 4, :].bitcast(I32))

        load_words(0)
        for q in range(4):
            nc.sync.dma_start(was_raw[32 * q:32 * q + 4, :, :].bitcast(I32),
                              wa4_scales[:, 4 * q:4 * q + 4, :].rearrange("a r c -> r a c").bitcast(I32))
        nc.sync.dma_start(wa_raw[:].bitcast(I32), wa4_words.rearrange("a p c -> p a c").bitcast(I32))
        load_ub_scales(0)
        load_words(1)
        load_ub_scales(1)
        load_ub_scales(2)

        def gather_words(a, j0, j1):
            nc.vector.tensor_copy(vw[a][:, j0:j1], tabw[a][:].bitcast(U32).indirect(idx[:, j0 // 16:j1 // 16]))

        def reorder(put, raw, words):
            nc.vector.tensor_copy(put.bitcast(I32).rearrange("p a (t g i) -> p a g t i", t=PACK, i=words),
                                  raw.bitcast(I32).rearrange("p a (g t i) -> p a g t i", t=PACK, i=words))

        def cast_wb(a, c0, c1, on_vector=False):
            dst = wb_bf[a][:].rearrange("p (t m j) -> p m t j", t=PACK, j=PACK)[:, c0 // PACK:c1 // PACK, :, :]
            src = wb_raw[a][:, :, c0:c1].rearrange("p j (m t) -> p m t j", t=PACK)
            if on_vector:
                nc.vector.tensor_copy(dst, src)
            else:
                nc.scalar.activation(dst, src, ACT.Copy)

        def bank_tile(k):
            return psum.tile([P, 512], F32, name="bank%d" % k)

        def quant_wb(a, c0, c1):
            nc.vector.quantize_mx(out=wb_w[a][:, c0:c1].bitcast(FP8X4), scales=wb_s[a][:, c0:c1],
                                  in_=wb_bf[a][:, PACK * c0:PACK * c1])

        def cast_ua(h, c0, c1, on_vector=False):
            dst = ua_bf[h][:, PACK * c0:PACK * c1].rearrange("p (c i j) -> p c j i", i=4, j=PACK)
            src = ua_raw[h][:, :, c0:c1].rearrange("p j (c i) -> p c j i", i=4)
            if on_vector:
                nc.vector.tensor_copy(dst, src)
            else:
                nc.scalar.activation(dst, src, ACT.Copy)

        def quant_ua(n0, n1):
            cols = slice(n0 * P, n1 * P)
            nc.vector.quantize_mx(out=ua_w[:, cols].bitcast(FP8X4), scales=ua_s[n0 // 2][:], in_=ua_bf[n0 // 2][:])

        def one_pass(b, jb, bank, a, t, first=0, last=PACK - 1):
            cols = slice(t * P, (t + 1) * P)
            js = slice(jb * JB, (jb + 1) * JB)
            if b == 0:
                lhs = wa_w[:, a, 2 * t * P:2 * (t + 1) * P].bitcast(FP4X4)
                lhs_s = wa_s[:, a, cols]
            else:
                lhs = wb_w[a][:, cols].bitcast(FP8X4)
                lhs_s = wb_s[a][:, cols]
            nc.tensor.matmul_mx(out=bank[:, cols], lhsT=lhs, lhsT_scale=lhs_s, rhs=vw[a][:, js].bitcast(FP8X4),
                                rhs_scale=vs[jb // 4][:, a, jb % 4 * JB:(jb % 4 + 1) * JB],
                                start=(a == first and t == 0), stop=(a == 1 - first and t == last))

        def h_bf(b, j0, j1):
            part, base = part_of(b, j0)
            return (h_a, h_b)[b][part][:, PACK * (j0 - base):PACK * (j1 - base)]

        def relu(b, jb, bank, on_vector=False):
            dst = h_bf(b, jb * JB, (jb + 1) * JB).rearrange("p (n t) -> p n t", t=PACK)
            src = bank[:].rearrange("p (t n) -> p n t", t=PACK)
            if on_vector:
                nc.vector.tensor_scalar_max(dst, src, 0.0)
            else:
                nc.scalar.activation(dst, src, ACT.Relu)

        def block(b, jb, k, first=0):
            bank = bank_tile(k)
            for a in (first, 1 - first):
                for t in range(PACK):
                    one_pass(b, jb, bank, a, t, first)
            return bank

        def quant_h(b, j0, j1):
            codes, scales = h_mx(b, j0, j1)
            nc.vector.quantize_mx(out=codes, scales=scales, in_=h_bf(b, j0, j1))

        def product(b, nt, j0, j1, dst):
            cols = slice(nt * P, (nt + 1) * P)
            if b == 0:
                u_w, u_s = ua_w[:, cols], ua_s[nt // 2][:, nt % 2 * P:(nt % 2 + 1) * P]
            else:
                u_w, u_s = ub_w[:, cols], ub_s[:, cols]
            codes, scales = h_mx(b, j0, j1)
            nc.tensor.matmul_mx(out=dst, lhsT=u_w.bitcast(FP8X4), lhsT_scale=u_s, rhs=codes, rhs_scale=scales,
                                start=True, stop=True)

        def value_pair(b, s, k):
            bank = bank_tile(k)
            for nt in range(2):
                product(b, nt, s * SP, (s + 1) * SP, bank[:, nt * SP:(nt + 1) * SP])
            return bank

        def value_half(b, nt, j0, k):
            bank = bank_tile(k)
            if b == 0 and j0 == 0:
                for c in range(2):
                    product(b, nt, c * SP, (c + 1) * SP, bank[:, c * SP:(c + 1) * SP])
            else:
                product(b, nt, j0, j0 + 2 * SP, bank[:])
            return bank

        def keep_a(nt, j0, k):
            nc.scalar.copy(ya_half[nt, j0][:], value_half(0, nt, j0, k)[:])

        def minimum(dst, bank, ya_sb):
            nc.vector.tensor_tensor(dst, bank, ya_sb, ALU.min)

        def min_pair(s, bank):
            for nt in range(2):
                cols = slice(nt * SP, (nt + 1) * SP)
                minimum(y_pair[s][:, cols], bank[:, cols], ya_pair[s][:, cols])

        def min_half(nt, j0, bank):
            minimum(y(nt, j0, j0 + 2 * SP), bank[:], ya_half[nt, j0][:])

        def scatter(nt, j0, j1):
            nc.vector.tensor_tensor(page[nt % 3][:].indirect(idx2[:, j0 // 16:j1 // 16]), y(nt, j0, j1),
                                    wgt[:, j0:j1], ALU.mult)

        def store(nt):
            if nt < 3:
                nc.sync.dma_start(out[nt * P:(nt + 1) * P, :], page[nt % 3][:])
                return
            for c, queue in enumerate((nc.sync, nc.scalar)):
                cols = slice(c * T2 // 2, (c + 1) * T2 // 2)
                queue.dma_start(out[nt * P:(nt + 1) * P, cols], page[nt % 3][:, cols])

        nc.vector.tensor_copy(vs_top[:], tabs[:].indirect(idx[:]))

        def move_scales(c):
            for a in range(2):
                for h in range(2):
                    p0 = 16 + 8 * a + 4 * h
                    nc.sync.dma_start(vs[c][64 * h:64 * h + 64, a, :].bitcast(I32),
                                      vs_top[p0:p0 + 64, c * S // 2:(c + 1) * S // 2].bitcast(I32))

        move_scales(0)
        load_wb(0, 0, H)
        load_wb(1, 0, H)
        gather_words(0, 0, S)
        load_ua(0)
        load_ub_scales(3)
        reorder(wa_w[:], wa_raw[:], 4)
        reorder(wa_s[:], was_raw[:], 2)
        nc.gpsimd.memset(page[2][:], 0.0)
        gather_words(1, 0, SP)
        gather_words(1, SP, 2 * SP)
        gather_words(1, 2 * SP, S)
        ub_words = ub8_words[0].rearrange("p c i -> p (c i)").bitcast(I32)
        nc.sync.dma_start(ub_w[:, 0:2 * P], ub_words[:, 0:2 * P])
        nc.sync.dma_start(wgt[:, 0:SP], wgo[:, 0:SP])
        nc.sync.dma_start(idx2[:], offs2)
        move_scales(1)
        load_ua(1)
        nc.sync.dma_start(wgt[:, SP:S], wgo[:, SP:S])
        nc.sync.dma_start(ub_w[:, 2 * P:N], ub_words[:, 2 * P:N])
        for jb in range(4):
            relu(0, jb, block(0, jb, 2 + jb, min(jb, 1)))
        cast_wb(0, 0, H, True)
        quant_h(0, 0, SP)
        quant_wb(0, 0, H)
        banks = [bank_tile(k) for k in (0, 1, 6, 7)]
        for jb in range(4):
            for t in range(PACK):
                one_pass(1, jb, banks[jb], 0, t)
        late_a = {}
        cast_wb(1, 0, CUT1)
        cast_wb(1, CUT1, H, True)
        for half in range(2):
            quant_wb(1, half * H // 2, (half + 1) * H // 2)
            for jb in range(2):
                for t in range(2 * half, 2 * half + 2):
                    one_pass(1, jb, banks[jb], 1, t)
        cast_ua(0, 0, P)
        cast_ua(0, P, 2 * P, True)
        quant_ua(0, 2)
        relu(1, 0, banks[0], True)
        relu(1, 1, banks[1])
        ya0 = value_pair(0, 0, 2)
        quant_h(1, 0, SP)
        yb0 = value_pair(1, 0, 4)
        nc.scalar.copy(ya_pair[0][:], ya0[:])
        quant_h(0, SP, 2 * SP)
        nc.scalar.copy(ya_pair[1][:], value_pair(0, 1, 3)[:])
        min_pair(0, yb0)
        scatter(0, 0, SP)
        scatter(1, 0, SP)
        for jb in range(2, 4):
            for t in (2, 3, 0, 1):
                one_pass(1, jb, banks[jb], 1, t, last=1)
            relu(1, jb, banks[jb])
        cast_ua(1, 0, 2 * P)
        for jb, k in ((4, 5), (5, 2), (6, 3), (7, 4)):
            late_a[jb] = block(0, jb, k)
        late_b = {4: block(1, 4, 6), 5: block(1, 5, 7)}
        for jb in range(4, 6):
            relu(0, jb, late_a[jb])
        quant_h(1, SP, 2 * SP)
        yb1 = value_pair(1, 1, 0)
        quant_ua(2, 4)
        quant_h(0, 2 * SP, 3 * SP)
        min_pair(1, yb1)
        scatter(0, SP, 2 * SP)
        scatter(1, SP, 2 * SP)
        for jb in range(6, 8):
            relu(0, jb, late_a[jb])
        late_b[6] = block(1, 6, 5)
        late_b[7] = block(1, 7, 2)
        for jb in range(4, 8):
            relu(1, jb, late_b[jb])
        keep_a(2, 0, 1)
        keep_a(3, 0, 3)
        yb20 = value_half(1, 2, 0, 4)
        yb30 = value_half(1, 3, 0, 6)
        quant_h(0, 3 * SP, S)
        for nt, k in enumerate((0, 7, 5, 2)):
            keep_a(nt, 2 * SP, k)
        quant_h(1, 2 * SP, S)
        min_half(2, 0, yb20)
        min_half(3, 0, yb30)
        for nt, k in enumerate((1, 3, 4, 6)):
            min_half(nt, 2 * SP, value_half(1, nt, 2 * SP, k))
        for nt in range(4):
            scatter(nt, 0 if nt >= 2 else 2 * SP, S)
            store(nt)
